import numpy as np
import ml_dtypes


def mxq(x, axis, fmt="e4m3"):
    dtype, down = {"e4m3": (ml_dtypes.float8_e4m3fn, 7), "e5m2": (ml_dtypes.float8_e5m2, 14)}[fmt]
    v = np.moveaxis(np.asarray(x, np.float32).astype(ml_dtypes.bfloat16).astype(np.float64), axis, -1)
    blocks = v.reshape(v.shape[:-1] + (-1, 32))
    amax = np.abs(blocks).max(-1, keepdims=True)
    byte = np.maximum(np.where(amax > 0, np.frexp(amax)[1] - 1 + 127, 0) - down, 1)
    scale = np.exp2(byte - 127.0)
    codes = (blocks / scale).astype(np.float32).astype(dtype).astype(np.float64)
    return np.moveaxis((codes * scale).reshape(v.shape), -1, axis)


WIDE = False


def mx_kscale(k):
    if not WIDE:
        return np.ones(k)
    levels = np.array([10, -10, 5, -5, 0])
    if k % 512:
        return np.exp2(np.random.permutation(np.resize(levels, k // 32))).repeat(32)
    a = np.empty((k // 512, 16))
    for p in range(k // 512):
        a[p, :8] = np.random.permutation(np.resize(levels, 8))
        for g in range(8):
            far = levels[np.abs(levels - a[p, g]) >= 10]
            a[p, g + 8] = far[np.random.randint(len(far))]
    return np.exp2(a.ravel()).repeat(32)


def f64(x):
    return np.asarray(x).astype(np.float64)


def striped(idx):
    return np.tile(idx.reshape(-1, 16).T, (8, 1)).astype(np.uint16)


def unstriped(offs):
    return offs[:16].T.reshape(-1).astype(np.int64)


def relu2(v):
    return np.maximum(v, 0.0) ** 2


K, T, E, C, N = 1536, 1536, 6, 256, 128


def by_expert(wq, xq):
    return np.concatenate([wq[e].T @ xq[:, e * C:(e + 1) * C] for e in range(E)], axis=1)


def setup_inputs():
    n = np.random.standard_normal
    s = mx_kscale(K)[:, None]
    return {
        "xT": (n((K, T)) * s).astype(np.float32),
        "w": (n((E, K, N)) / np.sqrt(K) / s[None]).astype(np.float32),
        "b": (0.3 * n((N, E))).astype(np.float32),
        "gate": np.tile(np.random.uniform(0.2, 1.0, E * C), (N, 1)).astype(np.float32),
        "offs": striped(np.random.permutation(T)[:E * C]),
        "dst": striped(np.random.permutation(T)[:E * C]),
    }


def reference(xT, w, b, gate, offs, dst):
    idx = unstriped(offs)
    xq = mxq(f64(xT)[:, idx], 0, "e4m3")
    y = by_expert(mxq(f64(w), 1, "e4m3"), xq)
    y = relu2(y + np.repeat(f64(b), C, axis=1))
    out = np.zeros((N, T))
    out[:, unstriped(dst)] = f64(gate) * y
    return out

@@ -1,0 +1,204 @@
+from contextlib import ExitStack
+
+import concourse.mybir as mybir
+
+K, T, E, C, N = 1536, 1536, 6, 256, 128
+FLOPS = 2 * E * C * K * N
+
+F32 = mybir.dt.float32
+BF16 = mybir.dt.bfloat16
+U32 = mybir.dt.uint32
+I32 = mybir.dt.int32
+U16 = mybir.dt.uint16
+U8 = mybir.dt.uint8
+FP8X4 = mybir.dt.float8_e4m3fn_x4
+ACT = mybir.ActivationFunctionType
+MULT = mybir.AluOpType.mult
+
+P = 128
+PACK = 4
+PASSES = K // (P * PACK)
+QUAD = 4
+HALF = T // 2
+WINDOW = 2048
+
+LOADS = (
+    (((512, 256), (512, 128)), ((512, 256),)),
+    (((512, 352), (512, 304)), ((512, 208),)),
+    (((512, 512),), ((512, 416),), ((256, 256),), ((256, 96),)),
+)
+GPSIMD_PASS = 2
+ADD = mybir.AluOpType.add
+
+
+def tile_moe_two_lin_relu2_kernel(tc, xT, w, b, gate, offs, dst, out):
+    nc = tc.nc
+    with ExitStack() as ctx:
+        held = ctx.enter_context(tc.tile_pool(name="held", bufs=1))
+        xraw = ctx.enter_context(tc.tile_pool(name="xraw", bufs=1))
+        xgrp = ctx.enter_context(tc.tile_pool(name="xgrp", bufs=3))
+        wraw = ctx.enter_context(tc.tile_pool(name="wraw", bufs=1))
+        psum = ctx.enter_context(tc.psum_pool(name="psum", bufs=1))
+
+        offs_sb = held.tile([P, T // 16], U16, name="offs_sb")
+        dst_sb = held.tile([P, T // 16], U16, name="dst_sb")
+        bias = held.tile([P, E], F32, name="bias")
+        gate_sb = held.tile([P, T], F32, name="gate_sb", align_bytes=64)
+        out_sb = held.tile([P, T], F32, name="out_sb", align_bytes=64)
+        planes = held.tile([P, T], U8, name="planes", align_bytes=64)
+        codes = [
+            held.tile([P, T if a == PASSES - 1 else WINDOW], U32, name=f"codes{a}", align_bytes=64)
+            for a in range(PASSES)
+        ]
+        g_codes = [held.tile([P, T], U32, name=f"g_codes{a}", align_bytes=64) for a in range(PASSES - 1)]
+        last_codes = []
+        g_planes = []
+        w_codes = held.tile([P, E, PASSES, N], U32, name="w_codes", align_bytes=64)
+        w_planes = held.tile([P, E, PASSES, N], U8, name="w_planes", align_bytes=64)
+        warm = held.tile([P, 1], F32, name="warm")
+
+        nc.gpsimd.memset(planes[:].bitcast(I32), 0)
+        for a in range(PASSES - 1):
+            nc.gpsimd.memset(codes[a][:, T:].bitcast(I32), 0)
+        nc.gpsimd.memset(warm[:], 0.0)
+        nc.scalar.activation(warm[:], warm[:], ACT.Relu)
+
+        pieces = [[] for a in range(PASSES)]
+        for a in range(PASSES):
+            rows = xT[a * 512 : (a + 1) * 512, :].rearrange("(p j) t -> p j t", j=PACK)
+            first = 0
+            for i, tiles in enumerate(LOADS[a]):
+                width = sum(cw for cw, ns in tiles)
+                raw = xraw.tile([P, PACK, width], F32, name=f"x{a}_{i}")
+                nc.sync.dma_start(out=raw[:], in_=rows[:, :, first : first + width])
+                lo = 0
+                for cw, ns in tiles:
+                    pieces[a].append((raw[:, :, lo : lo + cw], first + lo, cw, ns))
+                    lo += cw
+                first += width
+            if a == 0:
+                nc.sync.dma_start(offs_sb[:], offs)
+        w_raw = []
+        for e in range(E):
+            t = wraw.tile([P, PASSES, PACK * N], F32, name=f"w{e}")
+            nc.sync.dma_start(out=t[:], in_=w[e].rearrange("(a p j) n -> p a (j n)", p=P, j=PACK))
+            w_raw.append(t)
+            if e == 0:
+                nc.sync.dma_start(dst_sb[:], dst)
+            if e == 3:
+                nc.sync.dma_start(out=bias[:], in_=b)
+                nc.sync.dma_start(out=gate_sb[:, : 2 * C], in_=gate[:, : 2 * C])
+        nc.sync.dma_start(out=gate_sb[:, 2 * C :], in_=gate[:, 2 * C :])
+
+        def gather_words(h):
+            t = held.tile([P, HALF], U32, name=f"last{h}", tag="words" if h else "last0", align_bytes=64)
+            nc.vector.tensor_copy(t[:], codes[PASSES - 1][:].indirect(offs_sb[:, h * 48 : h * 48 + 48]))
+            last_codes.append(t)
+
+        def gather_bytes(h):
+            t = held.tile([P, HALF], U8, name=f"planes{h}", tag="bytes" if h else "planes0", align_bytes=64)
+            nc.vector.tensor_copy(t[:], planes[:].indirect(offs_sb[:, h * 48 : h * 48 + 48]))
+            g_planes.append(t)
+
+        for a in range(PASSES):
+            for src, c0, cw, ns in pieces[a]:
+                grp = xgrp.tile([P, cw, PACK], BF16, name=f"grp{cw}", align_bytes=64)
+                to = grp[:].rearrange("p (c i) t -> p c t i", i=4)
+                fr = src.rearrange("p t (c i) -> p c t i", i=4)
+                mid = ns // 4
+                nc.scalar.activation(to[:, :mid], fr[:, :mid], ACT.Copy)
+                if ns < cw:
+                    nc.vector.tensor_copy(to[:, mid:], fr[:, mid:])
+                nc.vector.quantize_mx(
+                    out=codes[a][:, c0 : c0 + cw].bitcast(FP8X4),
+                    scales=planes[QUAD * a : P, c0 : c0 + cw],
+                    in_=grp[:].rearrange("p w t -> p (w t)"),
+                )
+            if a < PASSES - 1:
+                nc.vector.tensor_copy(g_codes[a][:], codes[a][:].indirect(offs_sb[:]))
+
+        flat_codes = w_codes[:].rearrange("p e a n -> p (e a n)")
+        flat_planes = w_planes[:].rearrange("p e a n -> p (e a n)")
+        w_grp = []
+        for g in range(E // 2):
+            big = held.tile([P, 4, N, PACK], BF16, name=f"w_big{g}", tag=f"big{g}" if g else "words", align_bytes=64)
+            small = held.tile([P, 2, N, PACK], BF16, name=f"w_small{g}", tag=f"small{g}" if g else "bytes", align_bytes=64)
+            w_grp.append((big, small))
+
+        def w_copy(e):
+            for a in range(PASSES):
+                unit = e % 2 * PASSES + a
+                tile = w_grp[e // 2][unit // 4]
+                to = tile[:, unit % 4].rearrange("p (c i) t -> p c t i", i=4)
+                fr = w_raw[e][:, a].rearrange("p (t c i) -> p c t i", t=PACK, i=4)
+                if a < PASSES - 1:
+                    nc.scalar.activation(to, fr, ACT.Copy)
+                elif e < E - 1:
+                    nc.gpsimd.tensor_scalar(to, fr, 1.0, 0.0, MULT, ADD)
+                else:
+                    nc.vector.tensor_copy(to, fr)
+
+        def w_quant(g):
+            lo = g * 2 * PASSES * N
+            for tile, width in zip(w_grp[g], (4 * N, 2 * N)):
+                nc.vector.quantize_mx(
+                    out=flat_codes[:, lo : lo + width].bitcast(FP8X4),
+                    scales=flat_planes[:, lo : lo + width],
+                    in_=tile[:].rearrange("p u n t -> p (u n t)"),
+                )
+                lo += width
+
+        relu = [held.tile([P, 2 * C], F32, name=f"relu{g}") for g in range(E // 2)]
+
+        def multiply(e):
+            acc = psum.tile([P, C], F32, name=f"acc{e}")
+            cols = slice(e * C, (e + 1) * C)
+            in_half = slice(e % 3 * C, (e % 3 + 1) * C)
+            for a in range(PASSES):
+                nc.tensor.matmul_mx(
+                    out=acc[:],
+                    lhsT=w_codes[:, e, a, :].bitcast(FP8X4),
+                    lhsT_scale=w_planes[:, e, a, :],
+                    rhs=(g_codes[a][:, cols] if a < PASSES - 1 else last_codes[e // 3][:, in_half]).bitcast(FP8X4),
+                    rhs_scale=g_planes[e // 3][QUAD * a : P, in_half],
+                    start=(a == 0),
+                    stop=(a == PASSES - 1),
+                )
+            half = e % 2 * C
+            nc.scalar.activation(relu[e // 2][:, half : half + C], acc[:], ACT.Relu, bias=bias[:, e : e + 1])
+
+        def square(g):
+            nc.scalar.activation(relu[g][:], relu[g][:], ACT.Square)
+
+        def scatter(g):
+            cols = slice(g * 2 * C, (g + 1) * 2 * C)
+            nc.vector.tensor_tensor(
+                out_sb[:].indirect(dst_sb[:, g * 32 : (g + 1) * 32]), relu[g][:], gate_sb[:, cols], MULT
+            )
+
+        w_copy(0)
+        w_copy(1)
+        gather_words(0)
+        gather_bytes(0)
+        w_quant(0)
+        w_copy(2)
+        w_copy(3)
+        w_copy(4)
+        gather_words(1)
+        gather_bytes(1)
+        w_quant(1)
+        multiply(0)
+        multiply(1)
+        square(0)
+        scatter(0)
+        w_copy(5)
+        w_quant(2)
+        multiply(2)
+        multiply(3)
+        square(1)
+        scatter(1)
+        multiply(4)
+        multiply(5)
+        square(2)
+        scatter(2)
+        nc.sync.dma_start(out=out, in_=out_sb[:])

@@ -27,8 +27,8 @@ LOADS = (
     (((512, 352), (512, 304)), ((512, 208),)),
     (((512, 512),), ((512, 416),), ((256, 256),), ((256, 96),)),
 )
-GPSIMD_PASS = 2
-ADD = mybir.AluOpType.add
+PAIRS = E * PASSES // 2
+SLOT = 2 * PACK * N * 4
 
 
 def tile_moe_two_lin_relu2_kernel(tc, xT, w, b, gate, offs, dst, out):
@@ -43,7 +43,7 @@ def tile_moe_two_lin_relu2_kernel(tc, xT, w, b, gate, offs, dst, out):
         offs_sb = held.tile([P, T // 16], U16, name="offs_sb")
         dst_sb = held.tile([P, T // 16], U16, name="dst_sb")
         bias = held.tile([P, E], F32, name="bias")
-        gate_sb = held.tile([P, T], F32, name="gate_sb", align_bytes=64)
+        gate_sb = [held.tile([P, n * C], F32, name=f"gate{i}", align_bytes=64) for i, n in enumerate((1, 1, 4))]
         out_sb = held.tile([P, T], F32, name="out_sb", align_bytes=64)
         planes = held.tile([P, T], U8, name="planes", align_bytes=64)
         codes = [
@@ -53,8 +53,10 @@ def tile_moe_two_lin_relu2_kernel(tc, xT, w, b, gate, offs, dst, out):
         g_codes = [held.tile([P, T], U32, name=f"g_codes{a}", align_bytes=64) for a in range(PASSES - 1)]
         last_codes = []
         g_planes = []
-        w_codes = held.tile([P, E, PASSES, N], U32, name="w_codes", align_bytes=64)
-        w_planes = held.tile([P, E, PASSES, N], U8, name="w_planes", align_bytes=64)
+        sizes = (4, 4, 4, 4, 2)
+        w_codes = [held.tile([P, n * N], U32, name=f"w_codes{g}", align_bytes=64) for g, n in enumerate(sizes)]
+        w_planes = [held.tile([P, n * N], U8, name=f"w_planes{g}", align_bytes=64) for g, n in enumerate(sizes)]
+        w_grp = [held.tile([P, n, N, PACK], BF16, name=f"w_grp{g}", align_bytes=64) for g, n in enumerate(sizes)]
         warm = held.tile([P, 1], F32, name="warm")
 
         nc.gpsimd.memset(planes[:].bitcast(I32), 0)
@@ -78,25 +80,35 @@ def tile_moe_two_lin_relu2_kernel(tc, xT, w, b, gate, offs, dst, out):
                 first += width
             if a == 0:
                 nc.sync.dma_start(offs_sb[:], offs)
+        w_rows = w.rearrange("e k n -> (e k) n")
         w_raw = []
-        for e in range(E):
-            t = wraw.tile([P, PASSES, PACK * N], F32, name=f"w{e}")
-            nc.sync.dma_start(out=t[:], in_=w[e].rearrange("(a p j) n -> p a (j n)", p=P, j=PACK))
+        for q in range(PAIRS):
+            t = wraw.tile([P, 2, PACK * N], F32, name=f"w{q}", offset=q * SLOT, align_bytes=64)
+            rows = w_rows[q * 1024 : (q + 1) * 1024, :]
+            nc.sync.dma_start(out=t[:], in_=rows.rearrange("(u p j) n -> p u (j n)", p=P, j=PACK))
             w_raw.append(t)
-            if e == 0:
-                nc.sync.dma_start(dst_sb[:], dst)
-            if e == 3:
+            if q == 1:
                 nc.sync.dma_start(out=bias[:], in_=b)
-                nc.sync.dma_start(out=gate_sb[:, : 2 * C], in_=gate[:, : 2 * C])
-        nc.sync.dma_start(out=gate_sb[:, 2 * C :], in_=gate[:, 2 * C :])
+            if q == 5:
+                nc.sync.dma_start(dst_sb[:], dst)
+                nc.sync.dma_start(out=gate_sb[0][:], in_=gate[:, :C])
+            if q == 7:
+                nc.sync.dma_start(out=gate_sb[1][:], in_=gate[:, C : 2 * C])
+        nc.sync.dma_start(out=gate_sb[2][:], in_=gate[:, 2 * C :])
 
         def gather_words(h):
-            t = held.tile([P, HALF], U32, name=f"last{h}", tag="words" if h else "last0", align_bytes=64)
+            if h:
+                t = wraw.tile([P, HALF], U32, name="last1", offset=1 * SLOT, align_bytes=64)
+            else:
+                t = held.tile([P, HALF], U32, name="last0", align_bytes=64)
             nc.vector.tensor_copy(t[:], codes[PASSES - 1][:].indirect(offs_sb[:, h * 48 : h * 48 + 48]))
             last_codes.append(t)
 
         def gather_bytes(h):
-            t = held.tile([P, HALF], U8, name=f"planes{h}", tag="bytes" if h else "planes0", align_bytes=64)
+            if h:
+                t = wraw.tile([P, HALF], U8, name="planes1", offset=3 * SLOT, align_bytes=64)
+            else:
+                t = held.tile([P, HALF], U8, name="planes0", align_bytes=64)
             nc.vector.tensor_copy(t[:], planes[:].indirect(offs_sb[:, h * 48 : h * 48 + 48]))
             g_planes.append(t)
 
@@ -117,88 +129,73 @@ def tile_moe_two_lin_relu2_kernel(tc, xT, w, b, gate, offs, dst, out):
             if a < PASSES - 1:
                 nc.vector.tensor_copy(g_codes[a][:], codes[a][:].indirect(offs_sb[:]))
 
-        flat_codes = w_codes[:].rearrange("p e a n -> p (e a n)")
-        flat_planes = w_planes[:].rearrange("p e a n -> p (e a n)")
-        w_grp = []
-        for g in range(E // 2):
-            big = held.tile([P, 4, N, PACK], BF16, name=f"w_big{g}", tag=f"big{g}" if g else "words", align_bytes=64)
-            small = held.tile([P, 2, N, PACK], BF16, name=f"w_small{g}", tag=f"small{g}" if g else "bytes", align_bytes=64)
-            w_grp.append((big, small))
-
-        def w_copy(e):
-            for a in range(PASSES):
-                unit = e % 2 * PASSES + a
-                tile = w_grp[e // 2][unit // 4]
-                to = tile[:, unit % 4].rearrange("p (c i) t -> p c t i", i=4)
-                fr = w_raw[e][:, a].rearrange("p (t c i) -> p c t i", t=PACK, i=4)
-                if a < PASSES - 1:
-                    nc.scalar.activation(to, fr, ACT.Copy)
-                elif e < E - 1:
-                    nc.gpsimd.tensor_scalar(to, fr, 1.0, 0.0, MULT, ADD)
-                else:
-                    nc.vector.tensor_copy(to, fr)
+        def w_copy(q):
+            to = w_grp[q // 2][:, q % 2 * 2 : q % 2 * 2 + 2].rearrange("p u (c i) t -> p u c t i", i=4)
+            fr = w_raw[q][:].rearrange("p u (t c i) -> p u c t i", t=PACK, i=4)
+            nc.scalar.copy(to, fr)
 
         def w_quant(g):
-            lo = g * 2 * PASSES * N
-            for tile, width in zip(w_grp[g], (4 * N, 2 * N)):
-                nc.vector.quantize_mx(
-                    out=flat_codes[:, lo : lo + width].bitcast(FP8X4),
-                    scales=flat_planes[:, lo : lo + width],
-                    in_=tile[:].rearrange("p u n t -> p (u n t)"),
-                )
-                lo += width
+            nc.vector.quantize_mx(
+                out=w_codes[g][:].bitcast(FP8X4),
+                scales=w_planes[g][:],
+                in_=w_grp[g][:].rearrange("p u n t -> p (u n t)"),
+            )
 
-        relu = [held.tile([P, 2 * C], F32, name=f"relu{g}") for g in range(E // 2)]
-
-        def multiply(e):
+        def multiply(e, to):
             acc = psum.tile([P, C], F32, name=f"acc{e}")
             cols = slice(e * C, (e + 1) * C)
             in_half = slice(e % 3 * C, (e % 3 + 1) * C)
             for a in range(PASSES):
+                g, u = divmod(e * PASSES + a, 4)
                 nc.tensor.matmul_mx(
                     out=acc[:],
-                    lhsT=w_codes[:, e, a, :].bitcast(FP8X4),
-                    lhsT_scale=w_planes[:, e, a, :],
+                    lhsT=w_codes[g][:, u * N : (u + 1) * N].bitcast(FP8X4),
+                    lhsT_scale=w_planes[g][:, u * N : (u + 1) * N],
                     rhs=(g_codes[a][:, cols] if a < PASSES - 1 else last_codes[e // 3][:, in_half]).bitcast(FP8X4),
                     rhs_scale=g_planes[e // 3][QUAD * a : P, in_half],
                     start=(a == 0),
                     stop=(a == PASSES - 1),
                 )
-            half = e % 2 * C
-            nc.scalar.activation(relu[e // 2][:, half : half + C], acc[:], ACT.Relu, bias=bias[:, e : e + 1])
+            nc.scalar.activation(to, acc[:], ACT.Relu, bias=bias[:, e : e + 1])
 
-        def square(g):
-            nc.scalar.activation(relu[g][:], relu[g][:], ACT.Square)
-
-        def scatter(g):
-            cols = slice(g * 2 * C, (g + 1) * 2 * C)
-            nc.vector.tensor_tensor(
-                out_sb[:].indirect(dst_sb[:, g * 32 : (g + 1) * 32]), relu[g][:], gate_sb[:, cols], MULT
+        def finish(relu, first, count, gates):
+            nc.scalar.activation(relu[:], relu[:], ACT.Square)
+            return lambda: nc.vector.tensor_tensor(
+                out_sb[:].indirect(dst_sb[:, first * 16 : (first + count) * 16]), relu[:], gates, MULT
             )
 
-        w_copy(0)
-        w_copy(1)
         gather_words(0)
         gather_bytes(0)
+        w_copy(0)
+        w_copy(1)
         w_quant(0)
+        gather_words(1)
         w_copy(2)
         w_copy(3)
-        w_copy(4)
-        gather_words(1)
-        gather_bytes(1)
         w_quant(1)
-        multiply(0)
-        multiply(1)
-        square(0)
-        scatter(0)
+        gather_bytes(1)
+        w_copy(4)
+        relu0 = wraw.tile([P, C], F32, name="relu0", offset=3 * SLOT + 1024, align_bytes=64)
+        multiply(0, relu0[:])
+        scatter = finish(relu0, 0, 1, gate_sb[0][:])
         w_copy(5)
         w_quant(2)
-        multiply(2)
-        multiply(3)
-        square(1)
-        scatter(1)
-        multiply(4)
-        multiply(5)
-        square(2)
-        scatter(2)
+        scatter()
+        w_copy(6)
+        relu1 = wraw.tile([P, C], F32, name="relu1", offset=5 * SLOT, align_bytes=64)
+        multiply(1, relu1[:])
+        scatter = finish(relu1, 1, 1, gate_sb[1][:])
+        w_copy(7)
+        w_quant(3)
+        scatter()
+        w_copy(8)
+        w_quant(4)
+        relu23 = wraw.tile([P, 2 * C], F32, name="relu23", offset=7 * SLOT, align_bytes=64)
+        multiply(2, relu23[:, :C])
+        multiply(3, relu23[:, C:])
+        finish(relu23, 2, 2, gate_sb[2][:, : 2 * C])()
+        relu45 = held.tile([P, 2 * C], F32, name="relu45")
+        multiply(4, relu45[:, :C])
+        multiply(5, relu45[:, C:])
+        finish(relu45, 4, 2, gate_sb[2][:, 2 * C :])()
         nc.sync.dma_start(out=out, in_=out_sb[:])

@@ -23,9 +23,9 @@ HALF = T // 2
 WINDOW = 2048
 
 LOADS = (
-    (((512, 256), (512, 128)), ((512, 256),)),
-    (((512, 352), (512, 304)), ((512, 208),)),
-    (((512, 512),), ((512, 416),), ((256, 256),), ((256, 96),)),
+    (((512, 0), (512, 512), (512, 128),),),
+    (((512, 512),), ((512, 512),), ((512, 320),),),
+    (((512, 512),), ((512, 384),), ((256, 256),), ((256, 96),),),
 )
 PAIRS = E * PASSES // 2
 SLOT = 2 * PACK * N * 4
@@ -36,7 +36,7 @@ def tile_moe_two_lin_relu2_kernel(tc, xT, w, b, gate, offs, dst, out):
     with ExitStack() as ctx:
         held = ctx.enter_context(tc.tile_pool(name="held", bufs=1))
         xraw = ctx.enter_context(tc.tile_pool(name="xraw", bufs=1))
-        xgrp = ctx.enter_context(tc.tile_pool(name="xgrp", bufs=3))
+        xgrp = ctx.enter_context(tc.tile_pool(name="xgrp", bufs=4))
         wraw = ctx.enter_context(tc.tile_pool(name="wraw", bufs=1))
         psum = ctx.enter_context(tc.psum_pool(name="psum", bufs=1))
 
@@ -118,7 +118,8 @@ def tile_moe_two_lin_relu2_kernel(tc, xT, w, b, gate, offs, dst, out):
                 to = grp[:].rearrange("p (c i) t -> p c t i", i=4)
                 fr = src.rearrange("p t (c i) -> p c t i", i=4)
                 mid = ns // 4
-                nc.scalar.activation(to[:, :mid], fr[:, :mid], ACT.Copy)
+                if ns:
+                    nc.scalar.activation(to[:, :mid], fr[:, :mid], ACT.Copy)
                 if ns < cw:
                     nc.vector.tensor_copy(to[:, mid:], fr[:, mid:])
                 nc.vector.quantize_mx(

@@ -23,7 +23,7 @@ HALF = T // 2
 WINDOW = 2048
 
 LOADS = (
-    (((512, 0), (512, 512), (512, 128),),),
+    (((512, 256), (512, 0), (512, 512),),),
     (((512, 512),), ((512, 512),), ((512, 320),),),
     (((512, 512),), ((512, 384),), ((256, 256),), ((256, 96),),),
 )
@@ -36,15 +36,15 @@ def tile_moe_two_lin_relu2_kernel(tc, xT, w, b, gate, offs, dst, out):
     with ExitStack() as ctx:
         held = ctx.enter_context(tc.tile_pool(name="held", bufs=1))
         xraw = ctx.enter_context(tc.tile_pool(name="xraw", bufs=1))
-        xgrp = ctx.enter_context(tc.tile_pool(name="xgrp", bufs=4))
+        xgrp = ctx.enter_context(tc.tile_pool(name="xgrp", bufs=5))
         wraw = ctx.enter_context(tc.tile_pool(name="wraw", bufs=1))
         psum = ctx.enter_context(tc.psum_pool(name="psum", bufs=1))
 
         offs_sb = held.tile([P, T // 16], U16, name="offs_sb")
         dst_sb = held.tile([P, T // 16], U16, name="dst_sb")
         bias = held.tile([P, E], F32, name="bias")
-        gate_sb = [held.tile([P, n * C], F32, name=f"gate{i}", align_bytes=64) for i, n in enumerate((1, 1, 4))]
-        out_sb = held.tile([P, T], F32, name="out_sb", align_bytes=64)
+        gate_sb = [held.tile([P, n * C], F32, name=f"gate{i}", align_bytes=256) for i, n in enumerate((1, 1, 4))]
+        out_sb = held.tile([P, T], F32, name="out_sb", align_bytes=256)
         planes = held.tile([P, T], U8, name="planes", align_bytes=64)
         codes = [
             held.tile([P, T if a == PASSES - 1 else WINDOW], U32, name=f"codes{a}", align_bytes=64)
@@ -56,9 +56,10 @@ def tile_moe_two_lin_relu2_kernel(tc, xT, w, b, gate, offs, dst, out):
         sizes = (4, 4, 4, 4, 2)
         w_codes = [held.tile([P, n * N], U32, name=f"w_codes{g}", align_bytes=64) for g, n in enumerate(sizes)]
         w_planes = [held.tile([P, n * N], U8, name=f"w_planes{g}", align_bytes=64) for g, n in enumerate(sizes)]
-        w_grp = [held.tile([P, n, N, PACK], BF16, name=f"w_grp{g}", align_bytes=64) for g, n in enumerate(sizes)]
+        w_grp = [held.tile([P, n, N, PACK], BF16, name=f"w_grp{g}", align_bytes=64) for g, n in enumerate(sizes) if g != 3]
         warm = held.tile([P, 1], F32, name="warm")
 
+        nc.scalar.dma_start(out=bias[:], in_=b)
         nc.gpsimd.memset(planes[:].bitcast(I32), 0)
         for a in range(PASSES - 1):
             nc.gpsimd.memset(codes[a][:, T:].bitcast(I32), 0)
@@ -71,8 +72,15 @@ def tile_moe_two_lin_relu2_kernel(tc, xT, w, b, gate, offs, dst, out):
             first = 0
             for i, tiles in enumerate(LOADS[a]):
                 width = sum(cw for cw, ns in tiles)
-                raw = xraw.tile([P, PACK, width], F32, name=f"x{a}_{i}")
-                nc.sync.dma_start(out=raw[:], in_=rows[:, :, first : first + width])
+                raw = xraw.tile([P, PACK, width], F32, name=f"x{a}_{i}", align_bytes=256)
+                if a == 0:
+                    run = rows.rearrange("p j t -> p (j t)")
+                    flat = raw[:].rearrange("p j t -> p (j t)")
+                    cut = (PACK - 1) * T + tiles[0][0]
+                    nc.sync.dma_start(out=flat[:, :cut], in_=run[:, :cut])
+                    nc.sync.dma_start(out=flat[:, cut:], in_=run[:, cut:])
+                else:
+                    nc.sync.dma_start(out=raw[:], in_=rows[:, :, first : first + width])
                 lo = 0
                 for cw, ns in tiles:
                     pieces[a].append((raw[:, :, lo : lo + cw], first + lo, cw, ns))
@@ -83,12 +91,10 @@ def tile_moe_two_lin_relu2_kernel(tc, xT, w, b, gate, offs, dst, out):
         w_rows = w.rearrange("e k n -> (e k) n")
         w_raw = []
         for q in range(PAIRS):
-            t = wraw.tile([P, 2, PACK * N], F32, name=f"w{q}", offset=q * SLOT, align_bytes=64)
+            t = wraw.tile([P, 2, PACK * N], F32, name=f"w{q}", offset=(q + (q > 3)) * SLOT, align_bytes=256)
             rows = w_rows[q * 1024 : (q + 1) * 1024, :]
             nc.sync.dma_start(out=t[:], in_=rows.rearrange("(u p j) n -> p u (j n)", p=P, j=PACK))
             w_raw.append(t)
-            if q == 1:
-                nc.sync.dma_start(out=bias[:], in_=b)
             if q == 5:
                 nc.sync.dma_start(dst_sb[:], dst)
                 nc.sync.dma_start(out=gate_sb[0][:], in_=gate[:, :C])
@@ -130,10 +136,13 @@ def tile_moe_two_lin_relu2_kernel(tc, xT, w, b, gate, offs, dst, out):
             if a < PASSES - 1:
                 nc.vector.tensor_copy(g_codes[a][:], codes[a][:].indirect(offs_sb[:]))
 
-        def w_copy(q):
+        def w_views(q):
             to = w_grp[q // 2][:, q % 2 * 2 : q % 2 * 2 + 2].rearrange("p u (c i) t -> p u c t i", i=4)
             fr = w_raw[q][:].rearrange("p u (t c i) -> p u c t i", t=PACK, i=4)
-            nc.scalar.copy(to, fr)
+            return to, fr
+
+        def w_copy(q):
+            nc.scalar.copy(*w_views(q))
 
         def w_quant(g):
             nc.vector.quantize_mx(
@@ -176,14 +185,18 @@ def tile_moe_two_lin_relu2_kernel(tc, xT, w, b, gate, offs, dst, out):
         w_quant(1)
         gather_bytes(1)
         w_copy(4)
-        relu0 = wraw.tile([P, C], F32, name="relu0", offset=3 * SLOT + 1024, align_bytes=64)
+        relu0 = wraw.tile([P, C], F32, name="relu0", offset=4 * SLOT - 512, align_bytes=64)
         multiply(0, relu0[:])
-        scatter = finish(relu0, 0, 1, gate_sb[0][:])
         w_copy(5)
         w_quant(2)
-        scatter()
-        w_copy(6)
-        relu1 = wraw.tile([P, C], F32, name="relu1", offset=5 * SLOT, align_bytes=64)
+        square0 = held.tile([P, C], F32, name="square0")
+        nc.scalar.activation(square0[:], relu0[:], ACT.Square)
+        nc.vector.tensor_tensor(out_sb[:].indirect(dst_sb[:, :16]), square0[:], gate_sb[0][:], MULT)
+        w_grp.insert(3, wraw.tile([P, 4, N, PACK], BF16, name="w_grp3", offset=4 * SLOT, align_bytes=64))
+        to, fr = w_views(6)
+        nc.scalar.copy(to[:, 0], fr[:, 0])
+        nc.vector.tensor_copy(to[:, 1], fr[:, 1])
+        relu1 = wraw.tile([P, C], F32, name="relu1", offset=6 * SLOT, align_bytes=64)
         multiply(1, relu1[:])
         scatter = finish(relu1, 1, 1, gate_sb[1][:])
         w_copy(7)
@@ -191,7 +204,7 @@ def tile_moe_two_lin_relu2_kernel(tc, xT, w, b, gate, offs, dst, out):
         scatter()
         w_copy(8)
         w_quant(4)
-        relu23 = wraw.tile([P, 2 * C], F32, name="relu23", offset=7 * SLOT, align_bytes=64)
+        relu23 = wraw.tile([P, 2 * C], F32, name="relu23", offset=8 * SLOT, align_bytes=64)
         multiply(2, relu23[:, :C])
         multiply(3, relu23[:, C:])
         finish(relu23, 2, 2, gate_sb[2][:, : 2 * C])()

@@ -24,8 +24,8 @@ WINDOW = 2048
 
 LOADS = (
     (((512, 256), (512, 0), (512, 512),),),
-    (((512, 512),), ((512, 512),), ((512, 320),),),
-    (((512, 512),), ((512, 384),), ((256, 256),), ((256, 96),),),
+    (((512, 512),), ((512, 512),), ((512, 384),),),
+    (((512, 512),), ((512, 384),), ((256, 256),), ((256, 128),),),
 )
 PAIRS = E * PASSES // 2
 SLOT = 2 * PACK * N * 4
@@ -194,8 +194,8 @@ def tile_moe_two_lin_relu2_kernel(tc, xT, w, b, gate, offs, dst, out):
         nc.vector.tensor_tensor(out_sb[:].indirect(dst_sb[:, :16]), square0[:], gate_sb[0][:], MULT)
         w_grp.insert(3, wraw.tile([P, 4, N, PACK], BF16, name="w_grp3", offset=4 * SLOT, align_bytes=64))
         to, fr = w_views(6)
-        nc.scalar.copy(to[:, 0], fr[:, 0])
-        nc.vector.tensor_copy(to[:, 1], fr[:, 1])
+        nc.scalar.copy(to[:, :, :8], fr[:, :, :8])
+        nc.vector.tensor_copy(to[:, :, 8:], fr[:, :, 8:])
         relu1 = wraw.tile([P, C], F32, name="relu1", offset=6 * SLOT, align_bytes=64)
         multiply(1, relu1[:])
         scatter = finish(relu1, 1, 1, gate_sb[1][:])

@@ -56,7 +56,7 @@ def tile_moe_two_lin_relu2_kernel(tc, xT, w, b, gate, offs, dst, out):
         sizes = (4, 4, 4, 4, 2)
         w_codes = [held.tile([P, n * N], U32, name=f"w_codes{g}", align_bytes=64) for g, n in enumerate(sizes)]
         w_planes = [held.tile([P, n * N], U8, name=f"w_planes{g}", align_bytes=64) for g, n in enumerate(sizes)]
-        w_grp = [held.tile([P, n, N, PACK], BF16, name=f"w_grp{g}", align_bytes=64) for g, n in enumerate(sizes) if g != 3]
+        w_grp = [held.tile([P, n, N, PACK], BF16, name=f"w_grp{g}", align_bytes=64) for g, n in enumerate(sizes) if g < 3]
         warm = held.tile([P, 1], F32, name="warm")
 
         nc.scalar.dma_start(out=bias[:], in_=b)
@@ -202,13 +202,16 @@ def tile_moe_two_lin_relu2_kernel(tc, xT, w, b, gate, offs, dst, out):
         w_copy(7)
         w_quant(3)
         scatter()
-        w_copy(8)
-        w_quant(4)
         relu23 = wraw.tile([P, 2 * C], F32, name="relu23", offset=8 * SLOT, align_bytes=64)
         multiply(2, relu23[:, :C])
         multiply(3, relu23[:, C:])
-        finish(relu23, 2, 2, gate_sb[2][:, : 2 * C])()
-        relu45 = held.tile([P, 2 * C], F32, name="relu45")
+        w_grp.append(wraw.tile([P, 2, N, PACK], BF16, name="w_grp4", offset=8 * SLOT + 2048, align_bytes=64))
+        w_copy(8)
+        w_quant(4)
+        square23 = wraw.tile([P, 2 * C], F32, name="square23", offset=9 * SLOT, align_bytes=64)
+        nc.scalar.activation(square23[:], relu23[:], ACT.Square)
+        nc.vector.tensor_tensor(out_sb[:].indirect(dst_sb[:, 32:64]), square23[:], gate_sb[2][:, : 2 * C], MULT)
+        relu45 = wraw.tile([P, 2 * C], F32, name="relu45", offset=8 * SLOT, align_bytes=64)
         multiply(4, relu45[:, :C])
         multiply(5, relu45[:, C:])
         finish(relu45, 4, 2, gate_sb[2][:, 2 * C :])()

@@ -29,6 +29,7 @@ LOADS = (
 )
 PAIRS = E * PASSES // 2
 SLOT = 2 * PACK * N * 4
+SINGLE = 6
 
 
 def tile_moe_two_lin_relu2_kernel(tc, xT, w, b, gate, offs, dst, out):
@@ -43,15 +44,11 @@ def tile_moe_two_lin_relu2_kernel(tc, xT, w, b, gate, offs, dst, out):
         offs_sb = held.tile([P, T // 16], U16, name="offs_sb")
         dst_sb = held.tile([P, T // 16], U16, name="dst_sb")
         bias = held.tile([P, E], F32, name="bias")
-        gate_sb = [held.tile([P, n * C], F32, name=f"gate{i}", align_bytes=256) for i, n in enumerate((1, 1, 4))]
+        gate_sb = [held.tile([P, n * C], F32, name=f"gate{i}", align_bytes=256) for i, n in enumerate((2, 4))]
         out_sb = held.tile([P, T], F32, name="out_sb", align_bytes=256)
         planes = held.tile([P, T], U8, name="planes", align_bytes=64)
-        codes = [
-            held.tile([P, T if a == PASSES - 1 else WINDOW], U32, name=f"codes{a}", align_bytes=64)
-            for a in range(PASSES)
-        ]
-        g_codes = [held.tile([P, T], U32, name=f"g_codes{a}", align_bytes=64) for a in range(PASSES - 1)]
-        last_codes = []
+        codes = [held.tile([P, WINDOW], U32, name=f"codes{a}", align_bytes=64) for a in range(PASSES)]
+        g_codes = [held.tile([P, T], U32, name=f"g_codes{a}", align_bytes=64) for a in range(PASSES)]
         g_planes = []
         sizes = (4, 4, 4, 4, 2)
         w_codes = [held.tile([P, n * N], U32, name=f"w_codes{g}", align_bytes=64) for g, n in enumerate(sizes)]
@@ -59,9 +56,8 @@ def tile_moe_two_lin_relu2_kernel(tc, xT, w, b, gate, offs, dst, out):
         w_grp = [held.tile([P, n, N, PACK], BF16, name=f"w_grp{g}", align_bytes=64) for g, n in enumerate(sizes) if g < 3]
         warm = held.tile([P, 1], F32, name="warm")
 
-        nc.scalar.dma_start(out=bias[:], in_=b)
         nc.gpsimd.memset(planes[:].bitcast(I32), 0)
-        for a in range(PASSES - 1):
+        for a in range(PASSES):
             nc.gpsimd.memset(codes[a][:, T:].bitcast(I32), 0)
         nc.gpsimd.memset(warm[:], 0.0)
         nc.scalar.activation(warm[:], warm[:], ACT.Relu)
@@ -91,31 +87,28 @@ def tile_moe_two_lin_relu2_kernel(tc, xT, w, b, gate, offs, dst, out):
         w_rows = w.rearrange("e k n -> (e k) n")
         w_raw = []
         for q in range(PAIRS):
-            t = wraw.tile([P, 2, PACK * N], F32, name=f"w{q}", offset=(q + (q > 3)) * SLOT, align_bytes=256)
-            rows = w_rows[q * 1024 : (q + 1) * 1024, :]
-            nc.sync.dma_start(out=t[:], in_=rows.rearrange("(u p j) n -> p u (j n)", p=P, j=PACK))
-            w_raw.append(t)
-            if q == 5:
+            rows = w_rows[q * 1024 : (q + 1) * 1024, :].rearrange("(u p j) n -> p u (j n)", p=P, j=PACK)
+            parts = []
+            for u, n in ((0, 1), (1, 1)) if q < SINGLE else ((0, 2),):
+                at = (q + (q > 4)) * SLOT + u * SLOT // 2
+                t = wraw.tile([P, n, PACK * N], F32, name=f"w{q}_{u}", offset=at, align_bytes=256)
+                nc.sync.dma_start(out=t[:], in_=rows[:, u : u + n])
+                parts.append((u, n, t))
+            w_raw.append(parts)
+            if q == 1:
+                nc.sync.dma_start(out=bias[:], in_=b)
+            if q == 6:
                 nc.sync.dma_start(dst_sb[:], dst)
-                nc.sync.dma_start(out=gate_sb[0][:], in_=gate[:, :C])
-            if q == 7:
-                nc.sync.dma_start(out=gate_sb[1][:], in_=gate[:, C : 2 * C])
-        nc.sync.dma_start(out=gate_sb[2][:], in_=gate[:, 2 * C :])
-
-        def gather_words(h):
-            if h:
-                t = wraw.tile([P, HALF], U32, name="last1", offset=1 * SLOT, align_bytes=64)
-            else:
-                t = held.tile([P, HALF], U32, name="last0", align_bytes=64)
-            nc.vector.tensor_copy(t[:], codes[PASSES - 1][:].indirect(offs_sb[:, h * 48 : h * 48 + 48]))
-            last_codes.append(t)
+                nc.sync.dma_start(out=gate_sb[0][:], in_=gate[:, : 2 * C])
+        nc.sync.dma_start(out=gate_sb[1][:], in_=gate[:, 2 * C :])
 
         def gather_bytes(h):
             if h:
-                t = wraw.tile([P, HALF], U8, name="planes1", offset=3 * SLOT, align_bytes=64)
+                t = wraw.tile([P, 4 * C], U8, name="planes1", offset=3 * SLOT + SLOT // 2, align_bytes=64)
+                nc.vector.tensor_copy(t[:], planes[:].indirect(offs_sb[:, 32:]))
             else:
-                t = held.tile([P, HALF], U8, name="planes0", align_bytes=64)
-            nc.vector.tensor_copy(t[:], planes[:].indirect(offs_sb[:, h * 48 : h * 48 + 48]))
+                t = held.tile([P, 2 * C], U8, name="planes0", align_bytes=64)
+                nc.vector.tensor_copy(t[:], planes[:].indirect(offs_sb[:, :32]))
             g_planes.append(t)
 
         for a in range(PASSES):
@@ -133,16 +126,18 @@ def tile_moe_two_lin_relu2_kernel(tc, xT, w, b, gate, offs, dst, out):
                     scales=planes[QUAD * a : P, c0 : c0 + cw],
                     in_=grp[:].rearrange("p w t -> p (w t)"),
                 )
-            if a < PASSES - 1:
+            if True:
                 nc.vector.tensor_copy(g_codes[a][:], codes[a][:].indirect(offs_sb[:]))
 
-        def w_views(q):
-            to = w_grp[q // 2][:, q % 2 * 2 : q % 2 * 2 + 2].rearrange("p u (c i) t -> p u c t i", i=4)
-            fr = w_raw[q][:].rearrange("p u (t c i) -> p u c t i", t=PACK, i=4)
+        def w_views(q, part=0):
+            u, n, raw = w_raw[q][part]
+            to = w_grp[q // 2][:, q % 2 * 2 + u : q % 2 * 2 + u + n].rearrange("p u (c i) t -> p u c t i", i=4)
+            fr = raw[:].rearrange("p u (t c i) -> p u c t i", t=PACK, i=4)
             return to, fr
 
         def w_copy(q):
-            nc.scalar.copy(*w_views(q))
+            for part in range(len(w_raw[q])):
+                nc.scalar.copy(*w_views(q, part))
 
         def w_quant(g):
             nc.vector.quantize_mx(
@@ -154,15 +149,16 @@ def tile_moe_two_lin_relu2_kernel(tc, xT, w, b, gate, offs, dst, out):
         def multiply(e, to):
             acc = psum.tile([P, C], F32, name=f"acc{e}")
             cols = slice(e * C, (e + 1) * C)
-            in_half = slice(e % 3 * C, (e % 3 + 1) * C)
+            h = min(e // 2, 1)
+            in_part = slice((e - 2 * h) * C, (e - 2 * h + 1) * C)
             for a in range(PASSES):
                 g, u = divmod(e * PASSES + a, 4)
                 nc.tensor.matmul_mx(
                     out=acc[:],
                     lhsT=w_codes[g][:, u * N : (u + 1) * N].bitcast(FP8X4),
                     lhsT_scale=w_planes[g][:, u * N : (u + 1) * N],
-                    rhs=(g_codes[a][:, cols] if a < PASSES - 1 else last_codes[e // 3][:, in_half]).bitcast(FP8X4),
-                    rhs_scale=g_planes[e // 3][QUAD * a : P, in_half],
+                    rhs=g_codes[a][:, cols].bitcast(FP8X4),
+                    rhs_scale=g_planes[h][QUAD * a : P, in_part],
                     start=(a == 0),
                     stop=(a == PASSES - 1),
                 )
@@ -174,45 +170,42 @@ def tile_moe_two_lin_relu2_kernel(tc, xT, w, b, gate, offs, dst, out):
                 out_sb[:].indirect(dst_sb[:, first * 16 : (first + count) * 16]), relu[:], gates, MULT
             )
 
-        gather_words(0)
         gather_bytes(0)
         w_copy(0)
         w_copy(1)
         w_quant(0)
-        gather_words(1)
         w_copy(2)
         w_copy(3)
         w_quant(1)
         gather_bytes(1)
         w_copy(4)
-        relu0 = wraw.tile([P, C], F32, name="relu0", offset=4 * SLOT - 512, align_bytes=64)
-        multiply(0, relu0[:])
         w_copy(5)
         w_quant(2)
-        square0 = held.tile([P, C], F32, name="square0")
-        nc.scalar.activation(square0[:], relu0[:], ACT.Square)
-        nc.vector.tensor_tensor(out_sb[:].indirect(dst_sb[:, :16]), square0[:], gate_sb[0][:], MULT)
-        w_grp.insert(3, wraw.tile([P, 4, N, PACK], BF16, name="w_grp3", offset=4 * SLOT, align_bytes=64))
-        to, fr = w_views(6)
-        nc.scalar.copy(to[:, :, :8], fr[:, :, :8])
-        nc.vector.tensor_copy(to[:, :, 8:], fr[:, :, 8:])
-        relu1 = wraw.tile([P, C], F32, name="relu1", offset=6 * SLOT, align_bytes=64)
+        relu0 = wraw.tile([P, C], F32, name="relu0", offset=5 * SLOT - 1024, align_bytes=64)
+        relu1 = wraw.tile([P, C], F32, name="relu1", offset=4 * SLOT + 1024, align_bytes=64)
+        multiply(0, relu0[:])
         multiply(1, relu1[:])
-        scatter = finish(relu1, 1, 1, gate_sb[1][:])
+        square01 = held.tile([P, 2 * C], F32, name="square01")
+        nc.scalar.activation(square01[:, :C], relu0[:], ACT.Square)
+        nc.scalar.activation(square01[:, C:], relu1[:], ACT.Square)
+        nc.vector.tensor_tensor(out_sb[:].indirect(dst_sb[:, :32]), square01[:], gate_sb[0][:], MULT)
+        w_grp.append(wraw.tile([P, 4, N, PACK], BF16, name="w_grp3", offset=5 * SLOT - 512, align_bytes=64))
+        w_grp.append(wraw.tile([P, 2, N, PACK], BF16, name="w_grp4", offset=4 * SLOT, align_bytes=64))
+        to, fr = w_views(8)
+        nc.vector.tensor_copy(to[:, 1:], fr[:, 1:])
+        w_copy(6)
         w_copy(7)
         w_quant(3)
-        scatter()
-        relu23 = wraw.tile([P, 2 * C], F32, name="relu23", offset=8 * SLOT, align_bytes=64)
+        relu23 = wraw.tile([P, 2 * C], F32, name="relu23", offset=7 * SLOT, align_bytes=64)
         multiply(2, relu23[:, :C])
         multiply(3, relu23[:, C:])
-        w_grp.append(wraw.tile([P, 2, N, PACK], BF16, name="w_grp4", offset=8 * SLOT + 2048, align_bytes=64))
-        w_copy(8)
+        nc.scalar.copy(to[:, :1], fr[:, :1])
         w_quant(4)
-        square23 = wraw.tile([P, 2 * C], F32, name="square23", offset=9 * SLOT, align_bytes=64)
+        square23 = wraw.tile([P, 2 * C], F32, name="square23", offset=8 * SLOT, align_bytes=64)
         nc.scalar.activation(square23[:], relu23[:], ACT.Square)
-        nc.vector.tensor_tensor(out_sb[:].indirect(dst_sb[:, 32:64]), square23[:], gate_sb[2][:, : 2 * C], MULT)
-        relu45 = wraw.tile([P, 2 * C], F32, name="relu45", offset=8 * SLOT, align_bytes=64)
+        nc.vector.tensor_tensor(out_sb[:].indirect(dst_sb[:, 32:64]), square23[:], gate_sb[1][:, : 2 * C], MULT)
+        relu45 = wraw.tile([P, 2 * C], F32, name="relu45", offset=7 * SLOT, align_bytes=64)
         multiply(4, relu45[:, :C])
         multiply(5, relu45[:, C:])
-        finish(relu45, 4, 2, gate_sb[2][:, 2 * C :])()
+        finish(relu45, 4, 2, gate_sb[1][:, 2 * C :])()
         nc.sync.dma_start(out=out, in_=out_sb[:])

@@ -17,19 +17,30 @@ MULT = mybir.AluOpType.mult
 
 P = 128
 PACK = 4
-PASSES = K // (P * PACK)
-QUAD = 4
-HALF = T // 2
+K_PASS = P * PACK
+PASSES = K // K_PASS
+SCALE_ROWS = 4
+LINE = 4
+LIST_COLS = C // 16
 WINDOW = 2048
 
-LOADS = (
-    (((512, 256), (512, 0), (512, 512),),),
-    (((512, 512),), ((512, 512),), ((512, 384),),),
-    (((512, 512),), ((512, 384),), ((256, 256),), ((256, 128),),),
+X_LOADS = (
+    (((512, 192), (512, 0), (256, 256), (256, 256)),),
+    (((512, 512),), ((512, 512),), ((256, 256), (256, 64))),
+    (((512, 512),), ((256, 256), (256, 128)), ((256, 256),), ((256, 96),)),
 )
-PAIRS = E * PASSES // 2
-SLOT = 2 * PACK * N * 4
-SINGLE = 6
+X_BUFS = 5
+
+UNITS = E * PASSES
+GROUPS = (4, 4, 4, 4, 2)
+SINGLE = 12
+UNIT_BYTES = PACK * N * 4
+GAP = 10
+EARLY = 2
+
+
+def unit_at(unit):
+    return (unit + 2 * (unit >= GAP)) * UNIT_BYTES
 
 
 def tile_moe_two_lin_relu2_kernel(tc, xT, w, b, gate, offs, dst, out):
@@ -37,37 +48,38 @@ def tile_moe_two_lin_relu2_kernel(tc, xT, w, b, gate, offs, dst, out):
     with ExitStack() as ctx:
         held = ctx.enter_context(tc.tile_pool(name="held", bufs=1))
         xraw = ctx.enter_context(tc.tile_pool(name="xraw", bufs=1))
-        xgrp = ctx.enter_context(tc.tile_pool(name="xgrp", bufs=5))
+        xgrp = ctx.enter_context(tc.tile_pool(name="xgrp", bufs=X_BUFS))
         wraw = ctx.enter_context(tc.tile_pool(name="wraw", bufs=1))
         psum = ctx.enter_context(tc.psum_pool(name="psum", bufs=1))
 
         offs_sb = held.tile([P, T // 16], U16, name="offs_sb")
         dst_sb = held.tile([P, T // 16], U16, name="dst_sb")
         bias = held.tile([P, E], F32, name="bias")
-        gate_sb = [held.tile([P, n * C], F32, name=f"gate{i}", align_bytes=256) for i, n in enumerate((2, 4))]
+        gate_early = held.tile([P, EARLY * C], F32, name="gate0", align_bytes=256)
+        gate_late = held.tile([P, (E - EARLY) * C], F32, name="gate1", align_bytes=256)
         out_sb = held.tile([P, T], F32, name="out_sb", align_bytes=256)
-        planes = held.tile([P, T], U8, name="planes", align_bytes=64)
-        codes = [held.tile([P, WINDOW], U32, name=f"codes{a}", align_bytes=64) for a in range(PASSES)]
-        g_codes = [held.tile([P, T], U32, name=f"g_codes{a}", align_bytes=64) for a in range(PASSES)]
-        g_planes = []
-        sizes = (4, 4, 4, 4, 2)
-        w_codes = [held.tile([P, n * N], U32, name=f"w_codes{g}", align_bytes=64) for g, n in enumerate(sizes)]
-        w_planes = [held.tile([P, n * N], U8, name=f"w_planes{g}", align_bytes=64) for g, n in enumerate(sizes)]
-        w_grp = [held.tile([P, n, N, PACK], BF16, name=f"w_grp{g}", align_bytes=64) for g, n in enumerate(sizes) if g < 3]
+        x_scales = held.tile([P, T], U8, name="planes", align_bytes=64)
+        x_words = [held.tile([P, WINDOW], U32, name=f"codes{a}", align_bytes=64) for a in range(PASSES)]
+        slot_words = [held.tile([P, T], U32, name=f"g_codes{a}", align_bytes=64) for a in range(PASSES)]
+        w_words = [held.tile([P, n * N], U32, name=f"w_codes{g}", align_bytes=64) for g, n in enumerate(GROUPS)]
+        w_scales = [held.tile([P, n * N], U8, name=f"w_planes{g}", align_bytes=64) for g, n in enumerate(GROUPS)]
+        w_woven = [
+            held.tile([P, n, N, PACK], BF16, name=f"w_grp{g}", align_bytes=64) for g, n in enumerate(GROUPS[:-2])
+        ]
         warm = held.tile([P, 1], F32, name="warm")
 
-        nc.gpsimd.memset(planes[:].bitcast(I32), 0)
+        nc.gpsimd.memset(x_scales[:].bitcast(I32), 0)
         for a in range(PASSES):
-            nc.gpsimd.memset(codes[a][:, T:].bitcast(I32), 0)
+            nc.gpsimd.memset(x_words[a][:, T:].bitcast(I32), 0)
         nc.gpsimd.memset(warm[:], 0.0)
         nc.scalar.activation(warm[:], warm[:], ACT.Relu)
 
-        pieces = [[] for a in range(PASSES)]
+        x_tiles = [[] for a in range(PASSES)]
         for a in range(PASSES):
-            rows = xT[a * 512 : (a + 1) * 512, :].rearrange("(p j) t -> p j t", j=PACK)
+            rows = xT[a * K_PASS : (a + 1) * K_PASS, :].rearrange("(p j) t -> p j t", j=PACK)
             first = 0
-            for i, tiles in enumerate(LOADS[a]):
-                width = sum(cw for cw, ns in tiles)
+            for i, tiles in enumerate(X_LOADS[a]):
+                width = sum(tokens for tokens, share in tiles)
                 raw = xraw.tile([P, PACK, width], F32, name=f"x{a}_{i}", align_bytes=256)
                 if a == 0:
                     run = rows.rearrange("p j t -> p (j t)")
@@ -78,134 +90,125 @@ def tile_moe_two_lin_relu2_kernel(tc, xT, w, b, gate, offs, dst, out):
                 else:
                     nc.sync.dma_start(out=raw[:], in_=rows[:, :, first : first + width])
                 lo = 0
-                for cw, ns in tiles:
-                    pieces[a].append((raw[:, :, lo : lo + cw], first + lo, cw, ns))
-                    lo += cw
+                for tokens, share in tiles:
+                    x_tiles[a].append((raw[:, :, lo : lo + tokens], first + lo, tokens, share))
+                    lo += tokens
                 first += width
             if a == 0:
                 nc.sync.dma_start(offs_sb[:], offs)
-        w_rows = w.rearrange("e k n -> (e k) n")
-        w_raw = []
-        for q in range(PAIRS):
-            rows = w_rows[q * 1024 : (q + 1) * 1024, :].rearrange("(u p j) n -> p u (j n)", p=P, j=PACK)
-            parts = []
-            for u, n in ((0, 1), (1, 1)) if q < SINGLE else ((0, 2),):
-                at = (q + (q > 4)) * SLOT + u * SLOT // 2
-                t = wraw.tile([P, n, PACK * N], F32, name=f"w{q}_{u}", offset=at, align_bytes=256)
-                nc.sync.dma_start(out=t[:], in_=rows[:, u : u + n])
-                parts.append((u, n, t))
-            w_raw.append(parts)
-            if q == 1:
-                nc.sync.dma_start(out=bias[:], in_=b)
-            if q == 6:
-                nc.sync.dma_start(dst_sb[:], dst)
-                nc.sync.dma_start(out=gate_sb[0][:], in_=gate[:, : 2 * C])
-        nc.sync.dma_start(out=gate_sb[1][:], in_=gate[:, 2 * C :])
 
-        def gather_bytes(h):
-            if h:
-                t = wraw.tile([P, 4 * C], U8, name="planes1", offset=3 * SLOT + SLOT // 2, align_bytes=64)
-                nc.vector.tensor_copy(t[:], planes[:].indirect(offs_sb[:, 32:]))
-            else:
-                t = held.tile([P, 2 * C], U8, name="planes0", align_bytes=64)
-                nc.vector.tensor_copy(t[:], planes[:].indirect(offs_sb[:, :32]))
-            g_planes.append(t)
+        w_units = w.rearrange("e (a p j) n -> p (e a) (j n)", p=P, j=PACK)
+        w_raw = {}
+        for unit in list(range(SINGLE)) + list(range(SINGLE, UNITS, 2)):
+            count = 1 if unit < SINGLE else 2
+            raw = wraw.tile([P, count, PACK * N], F32, name=f"w{unit}", offset=unit_at(unit), align_bytes=256)
+            nc.sync.dma_start(out=raw[:], in_=w_units[:, unit : unit + count])
+            w_raw[unit] = raw
+            if unit + count == GROUPS[0]:
+                nc.sync.dma_start(out=bias[:], in_=b)
+            if unit == SINGLE:
+                nc.sync.dma_start(dst_sb[:], dst)
+                nc.sync.dma_start(out=gate_early[:], in_=gate[:, : EARLY * C])
+        nc.sync.dma_start(out=gate_late[:], in_=gate[:, EARLY * C :])
 
         for a in range(PASSES):
-            for src, c0, cw, ns in pieces[a]:
-                grp = xgrp.tile([P, cw, PACK], BF16, name=f"grp{cw}", align_bytes=64)
-                to = grp[:].rearrange("p (c i) t -> p c t i", i=4)
-                fr = src.rearrange("p t (c i) -> p c t i", i=4)
-                mid = ns // 4
-                if ns:
+            for src, first, tokens, share in x_tiles[a]:
+                woven = xgrp.tile([P, tokens, PACK], BF16, name=f"grp{tokens}", align_bytes=64)
+                to = woven[:].rearrange("p (c i) j -> p c j i", i=LINE)
+                fr = src.rearrange("p j (c i) -> p c j i", i=LINE)
+                mid = share // LINE
+                if share:
                     nc.scalar.activation(to[:, :mid], fr[:, :mid], ACT.Copy)
-                if ns < cw:
+                if share < tokens:
                     nc.vector.tensor_copy(to[:, mid:], fr[:, mid:])
                 nc.vector.quantize_mx(
-                    out=codes[a][:, c0 : c0 + cw].bitcast(FP8X4),
-                    scales=planes[QUAD * a : P, c0 : c0 + cw],
-                    in_=grp[:].rearrange("p w t -> p (w t)"),
+                    out=x_words[a][:, first : first + tokens].bitcast(FP8X4),
+                    scales=x_scales[SCALE_ROWS * a : P, first : first + tokens],
+                    in_=woven[:].rearrange("p t j -> p (t j)"),
                 )
-            if True:
-                nc.vector.tensor_copy(g_codes[a][:], codes[a][:].indirect(offs_sb[:]))
+            nc.vector.tensor_copy(slot_words[a][:], x_words[a][:].indirect(offs_sb[:]))
 
-        def w_views(q, part=0):
-            u, n, raw = w_raw[q][part]
-            to = w_grp[q // 2][:, q % 2 * 2 + u : q % 2 * 2 + u + n].rearrange("p u (c i) t -> p u c t i", i=4)
-            fr = raw[:].rearrange("p u (t c i) -> p u c t i", t=PACK, i=4)
+        def weave_views(unit):
+            g, u = divmod(unit, GROUPS[0])
+            count = w_raw[unit].shape[1]
+            to = w_woven[g][:, u : u + count].rearrange("p u (c i) j -> p u c j i", i=LINE)
+            fr = w_raw[unit][:].rearrange("p u (j c i) -> p u c j i", j=PACK, i=LINE)
             return to, fr
 
-        def w_copy(q):
-            for part in range(len(w_raw[q])):
-                nc.scalar.copy(*w_views(q, part))
+        def weave_group(g):
+            for unit in w_raw:
+                if unit // GROUPS[0] == g:
+                    nc.scalar.copy(*weave_views(unit))
 
-        def w_quant(g):
+        def quantise_group(g):
             nc.vector.quantize_mx(
-                out=w_codes[g][:].bitcast(FP8X4),
-                scales=w_planes[g][:],
-                in_=w_grp[g][:].rearrange("p u n t -> p (u n t)"),
+                out=w_words[g][:].bitcast(FP8X4),
+                scales=w_scales[g][:],
+                in_=w_woven[g][:].rearrange("p u n j -> p (u n j)"),
             )
 
-        def multiply(e, to):
+        def relu(e, to, scales):
             acc = psum.tile([P, C], F32, name=f"acc{e}")
-            cols = slice(e * C, (e + 1) * C)
-            h = min(e // 2, 1)
-            in_part = slice((e - 2 * h) * C, (e - 2 * h + 1) * C)
             for a in range(PASSES):
-                g, u = divmod(e * PASSES + a, 4)
+                g, u = divmod(e * PASSES + a, GROUPS[0])
                 nc.tensor.matmul_mx(
                     out=acc[:],
-                    lhsT=w_codes[g][:, u * N : (u + 1) * N].bitcast(FP8X4),
-                    lhsT_scale=w_planes[g][:, u * N : (u + 1) * N],
-                    rhs=g_codes[a][:, cols].bitcast(FP8X4),
-                    rhs_scale=g_planes[h][QUAD * a : P, in_part],
+                    lhsT=w_words[g][:, u * N : (u + 1) * N].bitcast(FP8X4),
+                    lhsT_scale=w_scales[g][:, u * N : (u + 1) * N],
+                    rhs=slot_words[a][:, e * C : (e + 1) * C].bitcast(FP8X4),
+                    rhs_scale=scales[SCALE_ROWS * a : P],
                     start=(a == 0),
                     stop=(a == PASSES - 1),
                 )
             nc.scalar.activation(to, acc[:], ACT.Relu, bias=bias[:, e : e + 1])
 
-        def finish(relu, first, count, gates):
-            nc.scalar.activation(relu[:], relu[:], ACT.Square)
-            return lambda: nc.vector.tensor_tensor(
-                out_sb[:].indirect(dst_sb[:, first * 16 : (first + count) * 16]), relu[:], gates, MULT
-            )
+        def scatter_pair(e, squares, gates):
+            places = dst_sb[:, e * LIST_COLS : (e + 2) * LIST_COLS]
+            nc.vector.tensor_tensor(out_sb[:].indirect(places), squares, gates, MULT)
 
-        gather_bytes(0)
-        w_copy(0)
-        w_copy(1)
-        w_quant(0)
-        w_copy(2)
-        w_copy(3)
-        w_quant(1)
-        gather_bytes(1)
-        w_copy(4)
-        w_copy(5)
-        w_quant(2)
-        relu0 = wraw.tile([P, C], F32, name="relu0", offset=5 * SLOT - 1024, align_bytes=64)
-        relu1 = wraw.tile([P, C], F32, name="relu1", offset=4 * SLOT + 1024, align_bytes=64)
-        multiply(0, relu0[:])
-        multiply(1, relu1[:])
+        def on_bytes(offset, columns, dtype, name):
+            return wraw.tile([P, columns], dtype, name=name, offset=offset, align_bytes=64)
+
+        scales_early = held.tile([P, EARLY * C], U8, name="planes0", align_bytes=64)
+        nc.vector.tensor_copy(scales_early[:], x_scales[:].indirect(offs_sb[:, : EARLY * LIST_COLS]))
+        for g in range(2):
+            weave_group(g)
+            quantise_group(g)
+        scales_late = on_bytes(unit_at(7), (E - EARLY) * C, U8, "planes1")
+        nc.vector.tensor_copy(scales_late[:], x_scales[:].indirect(offs_sb[:, EARLY * LIST_COLS :]))
+        weave_group(2)
+        quantise_group(2)
+
+        relu_bytes = C * 4
+        relu0 = on_bytes(unit_at(9) + UNIT_BYTES - relu_bytes, C, F32, "relu0")
+        relu1 = on_bytes(unit_at(8) + UNIT_BYTES - relu_bytes, C, F32, "relu1")
+        relu(0, relu0[:], scales_early[:, :C])
+        relu(1, relu1[:], scales_early[:, C:])
         square01 = held.tile([P, 2 * C], F32, name="square01")
         nc.scalar.activation(square01[:, :C], relu0[:], ACT.Square)
         nc.scalar.activation(square01[:, C:], relu1[:], ACT.Square)
-        nc.vector.tensor_tensor(out_sb[:].indirect(dst_sb[:, :32]), square01[:], gate_sb[0][:], MULT)
-        w_grp.append(wraw.tile([P, 4, N, PACK], BF16, name="w_grp3", offset=5 * SLOT - 512, align_bytes=64))
-        w_grp.append(wraw.tile([P, 2, N, PACK], BF16, name="w_grp4", offset=4 * SLOT, align_bytes=64))
-        to, fr = w_views(8)
-        nc.vector.tensor_copy(to[:, 1:], fr[:, 1:])
-        w_copy(6)
-        w_copy(7)
-        w_quant(3)
-        relu23 = wraw.tile([P, 2 * C], F32, name="relu23", offset=7 * SLOT, align_bytes=64)
-        multiply(2, relu23[:, :C])
-        multiply(3, relu23[:, C:])
-        nc.scalar.copy(to[:, :1], fr[:, :1])
-        w_quant(4)
-        square23 = wraw.tile([P, 2 * C], F32, name="square23", offset=8 * SLOT, align_bytes=64)
+        scatter_pair(0, square01[:], gate_early[:])
+
+        group3_at = unit_at(9) + UNIT_BYTES - relu_bytes // 2
+        w_woven.append(wraw.tile([P, GROUPS[3], N, PACK], BF16, name="w_grp3", offset=group3_at, align_bytes=64))
+        w_woven.append(wraw.tile([P, GROUPS[4], N, PACK], BF16, name="w_grp4", offset=unit_at(8), align_bytes=64))
+        last_to, last_fr = weave_views(UNITS - 2)
+        nc.vector.tensor_copy(last_to[:, 1:], last_fr[:, 1:])
+        weave_group(3)
+        quantise_group(3)
+
+        relu23 = on_bytes(unit_at(12), 2 * C, F32, "relu23")
+        relu(2, relu23[:, :C], scales_late[:, :C])
+        relu(3, relu23[:, C:], scales_late[:, C : 2 * C])
+        nc.scalar.copy(last_to[:, :1], last_fr[:, :1])
+        quantise_group(4)
+        square23 = on_bytes(unit_at(14), 2 * C, F32, "square23")
         nc.scalar.activation(square23[:], relu23[:], ACT.Square)
-        nc.vector.tensor_tensor(out_sb[:].indirect(dst_sb[:, 32:64]), square23[:], gate_sb[1][:, : 2 * C], MULT)
-        relu45 = wraw.tile([P, 2 * C], F32, name="relu45", offset=7 * SLOT, align_bytes=64)
-        multiply(4, relu45[:, :C])
-        multiply(5, relu45[:, C:])
-        finish(relu45, 4, 2, gate_sb[1][:, 2 * C :])()
+        scatter_pair(2, square23[:], gate_late[:, : 2 * C])
+
+        relu45 = on_bytes(unit_at(12), 2 * C, F32, "relu45")
+        relu(4, relu45[:, :C], scales_late[:, 2 * C : 3 * C])
+        relu(5, relu45[:, C:], scales_late[:, 3 * C :])
+        nc.scalar.activation(relu45[:], relu45[:], ACT.Square)
+        scatter_pair(4, relu45[:], gate_late[:, 2 * C :])
         nc.sync.dma_start(out=out, in_=out_sb[:])

@@ -32,15 +32,11 @@ X_LOADS = (
 X_BUFS = 5
 
 UNITS = E * PASSES
-GROUPS = (4, 4, 4, 4, 2)
-SINGLE = 12
 UNIT_BYTES = PACK * N * 4
-GAP = 10
 EARLY = 2
-
-
-def unit_at(unit):
-    return (unit + 2 * (unit >= GAP)) * UNIT_BYTES
+ON_VECTOR = 12
+OUT_PIECES = (512, 512, 512)
+ADD = mybir.AluOpType.add
 
 
 def tile_moe_two_lin_relu2_kernel(tc, xT, w, b, gate, offs, dst, out):
@@ -55,22 +51,24 @@ def tile_moe_two_lin_relu2_kernel(tc, xT, w, b, gate, offs, dst, out):
         offs_sb = held.tile([P, T // 16], U16, name="offs_sb")
         dst_sb = held.tile([P, T // 16], U16, name="dst_sb")
         bias = held.tile([P, E], F32, name="bias")
-        gate_early = held.tile([P, EARLY * C], F32, name="gate0", align_bytes=256)
-        gate_late = held.tile([P, (E - EARLY) * C], F32, name="gate1", align_bytes=256)
-        out_sb = held.tile([P, T], F32, name="out_sb", align_bytes=256)
+        gate_first = held.tile([P, C], F32, name="gate0", align_bytes=256)
+        gate_mid = held.tile([P, 3 * C], F32, name="gate1", align_bytes=256)
+        gate_last = held.tile([P, 2 * C], F32, name="gate2", align_bytes=256)
+        out_v = held.tile([P, T], F32, name="out_v", align_bytes=256)
+        out_s = held.tile([P, T], F32, name="out_s", align_bytes=256)
         x_scales = held.tile([P, T], U8, name="planes", align_bytes=64)
         x_words = [held.tile([P, WINDOW], U32, name=f"codes{a}", align_bytes=64) for a in range(PASSES)]
         slot_words = [held.tile([P, T], U32, name=f"g_codes{a}", align_bytes=64) for a in range(PASSES)]
-        w_words = [held.tile([P, n * N], U32, name=f"w_codes{g}", align_bytes=64) for g, n in enumerate(GROUPS)]
-        w_scales = [held.tile([P, n * N], U8, name=f"w_planes{g}", align_bytes=64) for g, n in enumerate(GROUPS)]
-        w_woven = [
-            held.tile([P, n, N, PACK], BF16, name=f"w_grp{g}", align_bytes=64) for g, n in enumerate(GROUPS[:-2])
-        ]
+        w_words = [held.tile([P, PASSES * N], U32, name=f"w_codes{e}", align_bytes=64) for e in range(E)]
+        w_scales = [held.tile([P, PASSES * N], U8, name=f"w_planes{e}", align_bytes=64) for e in range(E)]
+        w_woven = [held.tile([P, PASSES, N, PACK], BF16, name=f"w_grp{e}", align_bytes=64) for e in range(E)]
         warm = held.tile([P, 1], F32, name="warm")
 
         nc.gpsimd.memset(x_scales[:].bitcast(I32), 0)
         for a in range(PASSES):
             nc.gpsimd.memset(x_words[a][:, T:].bitcast(I32), 0)
+        nc.vector.memset(out_v[:], 0.0)
+        nc.vector.memset(out_s[:], 0.0)
         nc.gpsimd.memset(warm[:], 0.0)
         nc.scalar.activation(warm[:], warm[:], ACT.Relu)
 
@@ -97,19 +95,20 @@ def tile_moe_two_lin_relu2_kernel(tc, xT, w, b, gate, offs, dst, out):
             if a == 0:
                 nc.sync.dma_start(offs_sb[:], offs)
 
+
         w_units = w.rearrange("e (a p j) n -> p (e a) (j n)", p=P, j=PACK)
-        w_raw = {}
-        for unit in list(range(SINGLE)) + list(range(SINGLE, UNITS, 2)):
-            count = 1 if unit < SINGLE else 2
-            raw = wraw.tile([P, count, PACK * N], F32, name=f"w{unit}", offset=unit_at(unit), align_bytes=256)
-            nc.sync.dma_start(out=raw[:], in_=w_units[:, unit : unit + count])
-            w_raw[unit] = raw
-            if unit + count == GROUPS[0]:
+        w_raw = []
+        for unit in range(UNITS):
+            raw = wraw.tile([P, PACK * N], F32, name=f"w{unit}", offset=unit * UNIT_BYTES, align_bytes=256)
+            nc.sync.dma_start(out=raw[:], in_=w_units[:, unit])
+            w_raw.append(raw)
+            if unit == 3:
                 nc.sync.dma_start(out=bias[:], in_=b)
-            if unit == SINGLE:
+            if unit == 11:
                 nc.sync.dma_start(dst_sb[:], dst)
-                nc.sync.dma_start(out=gate_early[:], in_=gate[:, : EARLY * C])
-        nc.sync.dma_start(out=gate_late[:], in_=gate[:, EARLY * C :])
+                nc.sync.dma_start(out=gate_first[:], in_=gate[:, :C])
+        nc.sync.dma_start(out=gate_mid[:], in_=gate[:, C : 4 * C])
+        nc.sync.dma_start(out=gate_last[:], in_=gate[:, 4 * C :])
 
         for a in range(PASSES):
             for src, first, tokens, share in x_tiles[a]:
@@ -128,87 +127,102 @@ def tile_moe_two_lin_relu2_kernel(tc, xT, w, b, gate, offs, dst, out):
                 )
             nc.vector.tensor_copy(slot_words[a][:], x_words[a][:].indirect(offs_sb[:]))
 
-        def weave_views(unit):
-            g, u = divmod(unit, GROUPS[0])
-            count = w_raw[unit].shape[1]
-            to = w_woven[g][:, u : u + count].rearrange("p u (c i) j -> p u c j i", i=LINE)
-            fr = w_raw[unit][:].rearrange("p u (j c i) -> p u c j i", j=PACK, i=LINE)
-            return to, fr
 
-        def weave_group(g):
-            for unit in w_raw:
-                if unit // GROUPS[0] == g:
-                    nc.scalar.copy(*weave_views(unit))
+        def weave(unit, copy):
+            e, a = divmod(unit, PASSES)
+            to = w_woven[e][:, a].rearrange("p (c i) j -> p c j i", i=LINE)
+            fr = w_raw[unit][:].rearrange("p (j c i) -> p c j i", j=PACK, i=LINE)
+            copy(to, fr)
 
-        def quantise_group(g):
+        def quantise(e):
             nc.vector.quantize_mx(
-                out=w_words[g][:].bitcast(FP8X4),
-                scales=w_scales[g][:],
-                in_=w_woven[g][:].rearrange("p u n j -> p (u n j)"),
+                out=w_words[e][:].bitcast(FP8X4),
+                scales=w_scales[e][:],
+                in_=w_woven[e][:].rearrange("p u n j -> p (u n j)"),
             )
 
-        def relu(e, to, scales):
-            acc = psum.tile([P, C], F32, name=f"acc{e}")
+        acc = [psum.tile([P, C], F32, name=f"acc{e}") for e in range(E)]
+
+        def product(e, scales):
             for a in range(PASSES):
-                g, u = divmod(e * PASSES + a, GROUPS[0])
                 nc.tensor.matmul_mx(
-                    out=acc[:],
-                    lhsT=w_words[g][:, u * N : (u + 1) * N].bitcast(FP8X4),
-                    lhsT_scale=w_scales[g][:, u * N : (u + 1) * N],
+                    out=acc[e][:],
+                    lhsT=w_words[e][:, a * N : (a + 1) * N].bitcast(FP8X4),
+                    lhsT_scale=w_scales[e][:, a * N : (a + 1) * N],
                     rhs=slot_words[a][:, e * C : (e + 1) * C].bitcast(FP8X4),
                     rhs_scale=scales[SCALE_ROWS * a : P],
                     start=(a == 0),
                     stop=(a == PASSES - 1),
                 )
-            nc.scalar.activation(to, acc[:], ACT.Relu, bias=bias[:, e : e + 1])
 
-        def scatter_pair(e, squares, gates):
-            places = dst_sb[:, e * LIST_COLS : (e + 2) * LIST_COLS]
-            nc.vector.tensor_tensor(out_sb[:].indirect(places), squares, gates, MULT)
+        def relu(e, to):
+            nc.scalar.activation(to, acc[e][:], ACT.Relu, bias=bias[:, e : e + 1])
+
+        def square(to, fr):
+            nc.scalar.activation(to, fr, ACT.Square)
+
+        def places(e, count):
+            return dst_sb[:, e * LIST_COLS : (e + count) * LIST_COLS]
 
         def on_bytes(offset, columns, dtype, name):
             return wraw.tile([P, columns], dtype, name=name, offset=offset, align_bytes=64)
 
+        half = UNIT_BYTES // 2
         scales_early = held.tile([P, EARLY * C], U8, name="planes0", align_bytes=64)
         nc.vector.tensor_copy(scales_early[:], x_scales[:].indirect(offs_sb[:, : EARLY * LIST_COLS]))
-        for g in range(2):
-            weave_group(g)
-            quantise_group(g)
-        scales_late = on_bytes(unit_at(7), (E - EARLY) * C, U8, "planes1")
+        for e in range(EARLY):
+            for a in range(PASSES):
+                weave(e * PASSES + a, nc.scalar.copy)
+            quantise(e)
+            product(e, scales_early[:, e * C : (e + 1) * C])
+        scales_late = on_bytes(5 * UNIT_BYTES, (E - EARLY) * C, U8, "planes1")
         nc.vector.tensor_copy(scales_late[:], x_scales[:].indirect(offs_sb[:, EARLY * LIST_COLS :]))
-        weave_group(2)
-        quantise_group(2)
+        for e in (2, 3):
+            for a in range(PASSES):
+                weave(e * PASSES + a, nc.scalar.copy)
+            quantise(e)
+            product(e, scales_late[:, (e - EARLY) * C : (e - EARLY + 1) * C])
+        weave(ON_VECTOR, nc.vector.tensor_copy)
 
-        relu_bytes = C * 4
-        relu0 = on_bytes(unit_at(9) + UNIT_BYTES - relu_bytes, C, F32, "relu0")
-        relu1 = on_bytes(unit_at(8) + UNIT_BYTES - relu_bytes, C, F32, "relu1")
-        relu(0, relu0[:], scales_early[:, :C])
-        relu(1, relu1[:], scales_early[:, C:])
-        square01 = held.tile([P, 2 * C], F32, name="square01")
-        nc.scalar.activation(square01[:, :C], relu0[:], ACT.Square)
-        nc.scalar.activation(square01[:, C:], relu1[:], ACT.Square)
-        scatter_pair(0, square01[:], gate_early[:])
+        relu0 = on_bytes(11 * UNIT_BYTES, C, F32, "relu0")
+        relu1 = on_bytes(11 * UNIT_BYTES + half, C, F32, "relu1")
+        relu(0, relu0[:])
+        relu(1, relu1[:])
+        square0 = on_bytes(0, C, F32, "square0")
+        square(square0[:], relu0[:])
+        nc.vector.tensor_tensor(out_v[:].indirect(places(0, 1)), square0[:], gate_first[:], MULT)
 
-        group3_at = unit_at(9) + UNIT_BYTES - relu_bytes // 2
-        w_woven.append(wraw.tile([P, GROUPS[3], N, PACK], BF16, name="w_grp3", offset=group3_at, align_bytes=64))
-        w_woven.append(wraw.tile([P, GROUPS[4], N, PACK], BF16, name="w_grp4", offset=unit_at(8), align_bytes=64))
-        last_to, last_fr = weave_views(UNITS - 2)
-        nc.vector.tensor_copy(last_to[:, 1:], last_fr[:, 1:])
-        weave_group(3)
-        quantise_group(3)
+        for unit in (13, 14):
+            weave(unit, nc.scalar.copy)
+        quantise(4)
+        product(4, scales_late[:, 2 * C : 3 * C])
+        for unit in (15, 16, 17):
+            weave(unit, nc.scalar.copy)
+        quantise(5)
+        product(5, scales_late[:, 3 * C :])
 
-        relu23 = on_bytes(unit_at(12), 2 * C, F32, "relu23")
-        relu(2, relu23[:, :C], scales_late[:, :C])
-        relu(3, relu23[:, C:], scales_late[:, C : 2 * C])
-        nc.scalar.copy(last_to[:, :1], last_fr[:, :1])
-        quantise_group(4)
-        square23 = on_bytes(unit_at(14), 2 * C, F32, "square23")
-        nc.scalar.activation(square23[:], relu23[:], ACT.Square)
-        scatter_pair(2, square23[:], gate_late[:, : 2 * C])
+        last = 17 * UNIT_BYTES
+        square1 = on_bytes(last - half + 256, C, F32, "square1")
+        square(square1[:], relu1[:])
+        nc.vector.tensor_tensor(out_v[:].indirect(places(1, 1)), square1[:], gate_mid[:, :C], MULT)
+        late = on_bytes(last + 256, 4 * C, F32, "late")
+        relu(2, late[:, :C])
+        relu(3, late[:, C : 2 * C])
+        square(late[:, :C], late[:, :C])
+        square(late[:, C : 2 * C], late[:, C : 2 * C])
+        gated = on_bytes(2 * UNIT_BYTES, 2 * C, F32, "gated")
+        nc.vector.tensor_tensor(gated[:], late[:, : 2 * C], gate_mid[:, C:], MULT)
+        relu(4, late[:, 2 * C : 3 * C])
+        relu(5, late[:, 3 * C :])
+        square(late[:, 2 * C : 3 * C], late[:, 2 * C : 3 * C])
+        square(late[:, 3 * C :], late[:, 3 * C :])
+        nc.vector.tensor_tensor(out_v[:].indirect(places(4, 2)), late[:, 2 * C :], gate_last[:], MULT)
+        for i in range(2):
+            nc.scalar.activation(out_s[:].indirect(places(2 + i, 1)), gated[:, i * C : (i + 1) * C], ACT.Copy)
 
-        relu45 = on_bytes(unit_at(12), 2 * C, F32, "relu45")
-        relu(4, relu45[:, :C], scales_late[:, 2 * C : 3 * C])
-        relu(5, relu45[:, C:], scales_late[:, 3 * C :])
-        nc.scalar.activation(relu45[:], relu45[:], ACT.Square)
-        scatter_pair(4, relu45[:], gate_late[:, 2 * C :])
-        nc.sync.dma_start(out=out, in_=out_sb[:])
+        first = 0
+        for width in OUT_PIECES:
+            piece = slice(first, first + width)
+            nc.vector.tensor_tensor(out_v[:, piece], out_v[:, piece], out_s[:, piece], ADD)
+            nc.sync.dma_start(out=out[:, piece], in_=out_v[:, piece])
+            first += width

@@ -34,6 +34,7 @@ X_BUFS = 5
 UNITS = E * PASSES
 UNIT_BYTES = PACK * N * 4
 EARLY = 2
+ON_GPSIMD = (3, 4)
 ON_VECTOR = 12
 OUT_PIECES = (512, 512, 512)
 ADD = mybir.AluOpType.add
@@ -134,6 +135,11 @@ def tile_moe_two_lin_relu2_kernel(tc, xT, w, b, gate, offs, dst, out):
             fr = w_raw[unit][:].rearrange("p (j c i) -> p c j i", j=PACK, i=LINE)
             copy(to, fr)
 
+        def weave_gpsimd(unit):
+            e, a = divmod(unit, PASSES)
+            fr = w_raw[unit][:].rearrange("p (j n) -> p n j", j=PACK)
+            nc.gpsimd.tensor_scalar(w_woven[e][:, a], fr, 1.0, 0.0, MULT, ADD)
+
         def quantise(e):
             nc.vector.quantize_mx(
                 out=w_words[e][:].bitcast(FP8X4),
@@ -171,11 +177,14 @@ def tile_moe_two_lin_relu2_kernel(tc, xT, w, b, gate, offs, dst, out):
         scales_early = held.tile([P, EARLY * C], U8, name="planes0", align_bytes=64)
         nc.vector.tensor_copy(scales_early[:], x_scales[:].indirect(offs_sb[:, : EARLY * LIST_COLS]))
         for e in range(EARLY):
-            for a in range(PASSES):
-                weave(e * PASSES + a, nc.scalar.copy)
+            for unit in range(e * PASSES, (e + 1) * PASSES):
+                if unit in ON_GPSIMD:
+                    weave_gpsimd(unit)
+                else:
+                    weave(unit, nc.scalar.copy)
             quantise(e)
             product(e, scales_early[:, e * C : (e + 1) * C])
-        scales_late = on_bytes(5 * UNIT_BYTES, (E - EARLY) * C, U8, "planes1")
+        scales_late = on_bytes(5 * UNIT_BYTES - 512, (E - EARLY) * C, U8, "planes1")
         nc.vector.tensor_copy(scales_late[:], x_scales[:].indirect(offs_sb[:, EARLY * LIST_COLS :]))
         for e in (2, 3):
             for a in range(PASSES):

@@ -33,9 +33,11 @@ X_BUFS = 5
 
 UNITS = E * PASSES
 UNIT_BYTES = PACK * N * 4
-EARLY = 2
 ON_GPSIMD = (3, 4)
-ON_VECTOR = 12
+ON_VECTOR = (17,)
+SECOND = 192
+SHARES = (288, 256)
+EARLY = 2
 OUT_PIECES = (512, 512, 512)
 ADD = mybir.AluOpType.add
 
@@ -46,23 +48,27 @@ def tile_moe_two_lin_relu2_kernel(tc, xT, w, b, gate, offs, dst, out):
         held = ctx.enter_context(tc.tile_pool(name="held", bufs=1))
         xraw = ctx.enter_context(tc.tile_pool(name="xraw", bufs=1))
         xgrp = ctx.enter_context(tc.tile_pool(name="xgrp", bufs=X_BUFS))
-        wraw = ctx.enter_context(tc.tile_pool(name="wraw", bufs=1))
+        shared = ctx.enter_context(tc.tile_pool(name="shared", bufs=1))
         psum = ctx.enter_context(tc.psum_pool(name="psum", bufs=1))
+
+        def on_bytes(offset, shape, dtype, name):
+            return shared.tile([P] + shape, dtype, name=name, offset=offset, align_bytes=64)
+
+        def on_unit(unit, shape, dtype, name):
+            return on_bytes(unit * UNIT_BYTES, shape, dtype, name)
+
 
         offs_sb = held.tile([P, T // 16], U16, name="offs_sb")
         dst_sb = held.tile([P, T // 16], U16, name="dst_sb")
         bias = held.tile([P, E], F32, name="bias")
-        gate_first = held.tile([P, C], F32, name="gate0", align_bytes=256)
-        gate_mid = held.tile([P, 3 * C], F32, name="gate1", align_bytes=256)
-        gate_last = held.tile([P, 2 * C], F32, name="gate2", align_bytes=256)
+        gate0 = held.tile([P, C], F32, name="gate0", align_bytes=256)
+        gate_mid = held.tile([P, SECOND + sum(SHARES)], F32, name="gate_mid", align_bytes=256)
+        gate_last = held.tile([P, 5 * C - SECOND - sum(SHARES)], F32, name="gate_last", align_bytes=256)
         out_v = held.tile([P, T], F32, name="out_v", align_bytes=256)
         out_s = held.tile([P, T], F32, name="out_s", align_bytes=256)
         x_scales = held.tile([P, T], U8, name="planes", align_bytes=64)
         x_words = [held.tile([P, WINDOW], U32, name=f"codes{a}", align_bytes=64) for a in range(PASSES)]
         slot_words = [held.tile([P, T], U32, name=f"g_codes{a}", align_bytes=64) for a in range(PASSES)]
-        w_words = [held.tile([P, PASSES * N], U32, name=f"w_codes{e}", align_bytes=64) for e in range(E)]
-        w_scales = [held.tile([P, PASSES * N], U8, name=f"w_planes{e}", align_bytes=64) for e in range(E)]
-        w_woven = [held.tile([P, PASSES, N, PACK], BF16, name=f"w_grp{e}", align_bytes=64) for e in range(E)]
         warm = held.tile([P, 1], F32, name="warm")
 
         nc.gpsimd.memset(x_scales[:].bitcast(I32), 0)
@@ -96,20 +102,19 @@ def tile_moe_two_lin_relu2_kernel(tc, xT, w, b, gate, offs, dst, out):
             if a == 0:
                 nc.sync.dma_start(offs_sb[:], offs)
 
-
         w_units = w.rearrange("e (a p j) n -> p (e a) (j n)", p=P, j=PACK)
         w_raw = []
         for unit in range(UNITS):
-            raw = wraw.tile([P, PACK * N], F32, name=f"w{unit}", offset=unit * UNIT_BYTES, align_bytes=256)
+            raw = on_unit(unit, [PACK * N], F32, f"w{unit}")
             nc.sync.dma_start(out=raw[:], in_=w_units[:, unit])
             w_raw.append(raw)
             if unit == 3:
                 nc.sync.dma_start(out=bias[:], in_=b)
             if unit == 11:
                 nc.sync.dma_start(dst_sb[:], dst)
-                nc.sync.dma_start(out=gate_first[:], in_=gate[:, :C])
-        nc.sync.dma_start(out=gate_mid[:], in_=gate[:, C : 4 * C])
-        nc.sync.dma_start(out=gate_last[:], in_=gate[:, 4 * C :])
+                nc.sync.dma_start(out=gate0[:], in_=gate[:, :C])
+        nc.sync.dma_start(out=gate_mid[:], in_=gate[:, C : C + SECOND + sum(SHARES)])
+        nc.sync.dma_start(out=gate_last[:], in_=gate[:, C + SECOND + sum(SHARES) :])
 
         for a in range(PASSES):
             for src, first, tokens, share in x_tiles[a]:
@@ -128,34 +133,39 @@ def tile_moe_two_lin_relu2_kernel(tc, xT, w, b, gate, offs, dst, out):
                 )
             nc.vector.tensor_copy(slot_words[a][:], x_words[a][:].indirect(offs_sb[:]))
 
+        w_woven = [held.tile([P, PASSES, N, PACK], BF16, name=f"w_grp{e}", align_bytes=64) for e in range(E)]
+        w_words = [held.tile([P, PASSES * N], U32, name=f"w_codes{e}", align_bytes=64) for e in range(E)]
+        w_scales = [held.tile([P, PASSES * N], U8, name=f"w_planes{e}", align_bytes=64) for e in range(E)]
 
-        def weave(unit, copy):
+        def weave(unit):
             e, a = divmod(unit, PASSES)
-            to = w_woven[e][:, a].rearrange("p (c i) j -> p c j i", i=LINE)
-            fr = w_raw[unit][:].rearrange("p (j c i) -> p c j i", j=PACK, i=LINE)
-            copy(to, fr)
-
-        def weave_gpsimd(unit):
-            e, a = divmod(unit, PASSES)
-            fr = w_raw[unit][:].rearrange("p (j n) -> p n j", j=PACK)
-            nc.gpsimd.tensor_scalar(w_woven[e][:, a], fr, 1.0, 0.0, MULT, ADD)
+            if unit in ON_GPSIMD:
+                fr = w_raw[unit][:].rearrange("p (j n) -> p n j", j=PACK)
+                nc.gpsimd.tensor_scalar(w_woven[e][:, a], fr, 1.0, 0.0, MULT, ADD)
+            else:
+                to = w_woven[e][:, a].rearrange("p (c i) j -> p c j i", i=LINE)
+                fr = w_raw[unit][:].rearrange("p (j c i) -> p c j i", j=PACK, i=LINE)
+                copy = nc.vector.tensor_copy if unit in ON_VECTOR else nc.scalar.copy
+                copy(to, fr)
 
         def quantise(e):
-            nc.vector.quantize_mx(
-                out=w_words[e][:].bitcast(FP8X4),
-                scales=w_scales[e][:],
-                in_=w_woven[e][:].rearrange("p u n j -> p (u n j)"),
-            )
+            for lo, hi in ((0, 2), (2, 3)) if e == E - 1 else ((0, 3),):
+                nc.vector.quantize_mx(
+                    out=w_words[e][:, lo * N : hi * N].bitcast(FP8X4),
+                    scales=w_scales[e][:, lo * N : hi * N],
+                    in_=w_woven[e][:, lo:hi].rearrange("p u n j -> p (u n j)"),
+                )
 
         acc = [psum.tile([P, C], F32, name=f"acc{e}") for e in range(E)]
 
         def product(e, scales):
             for a in range(PASSES):
+                words = slot_words[a][:, e * C : (e + 1) * C]
                 nc.tensor.matmul_mx(
                     out=acc[e][:],
                     lhsT=w_words[e][:, a * N : (a + 1) * N].bitcast(FP8X4),
                     lhsT_scale=w_scales[e][:, a * N : (a + 1) * N],
-                    rhs=slot_words[a][:, e * C : (e + 1) * C].bitcast(FP8X4),
+                    rhs=words.bitcast(FP8X4),
                     rhs_scale=scales[SCALE_ROWS * a : P],
                     start=(a == 0),
                     stop=(a == PASSES - 1),
@@ -167,67 +177,61 @@ def tile_moe_two_lin_relu2_kernel(tc, xT, w, b, gate, offs, dst, out):
         def square(to, fr):
             nc.scalar.activation(to, fr, ACT.Square)
 
-        def places(e, count):
-            return dst_sb[:, e * LIST_COLS : (e + count) * LIST_COLS]
+        def entries(lists, first, count):
+            return lists[:, first // 16 : (first + count) // 16]
 
-        def on_bytes(offset, columns, dtype, name):
-            return wraw.tile([P, columns], dtype, name=name, offset=offset, align_bytes=64)
+        def gather(to, window, first, count):
+            nc.vector.tensor_copy(to, window[:].indirect(entries(offs_sb, first, count)))
 
-        half = UNIT_BYTES // 2
-        scales_early = held.tile([P, EARLY * C], U8, name="planes0", align_bytes=64)
-        nc.vector.tensor_copy(scales_early[:], x_scales[:].indirect(offs_sb[:, : EARLY * LIST_COLS]))
+        def scatter_gated(first, count, values, gates):
+            nc.vector.tensor_tensor(out_v[:].indirect(entries(dst_sb, first, count)), values, gates, MULT)
+
+        def scatter_plain(first, count, values):
+            nc.scalar.activation(out_s[:].indirect(entries(dst_sb, first, count)), values, ACT.Copy)
+
+        scales_early = held.tile([P, EARLY * C], U8, name="scales_early", align_bytes=64)
+        gather(scales_early[:], x_scales, 0, EARLY * C)
         for e in range(EARLY):
             for unit in range(e * PASSES, (e + 1) * PASSES):
-                if unit in ON_GPSIMD:
-                    weave_gpsimd(unit)
-                else:
-                    weave(unit, nc.scalar.copy)
+                weave(unit)
             quantise(e)
             product(e, scales_early[:, e * C : (e + 1) * C])
-        scales_late = on_bytes(5 * UNIT_BYTES - 512, (E - EARLY) * C, U8, "planes1")
-        nc.vector.tensor_copy(scales_late[:], x_scales[:].indirect(offs_sb[:, EARLY * LIST_COLS :]))
-        for e in (2, 3):
-            for a in range(PASSES):
-                weave(e * PASSES + a, nc.scalar.copy)
+        scales_late = on_bytes(5 * UNIT_BYTES - 512, [(E - EARLY) * C], U8, "scales_late")
+        gather(scales_late[:], x_scales, EARLY * C, (E - EARLY) * C)
+
+        def late_product(e):
+            for unit in range(e * PASSES, (e + 1) * PASSES):
+                weave(unit)
             quantise(e)
             product(e, scales_late[:, (e - EARLY) * C : (e - EARLY + 1) * C])
-        weave(ON_VECTOR, nc.vector.tensor_copy)
 
-        relu0 = on_bytes(11 * UNIT_BYTES, C, F32, "relu0")
-        relu1 = on_bytes(11 * UNIT_BYTES + half, C, F32, "relu1")
-        relu(0, relu0[:])
-        relu(1, relu1[:])
-        square0 = on_bytes(0, C, F32, "square0")
-        square(square0[:], relu0[:])
-        nc.vector.tensor_tensor(out_v[:].indirect(places(0, 1)), square0[:], gate_first[:], MULT)
-
-        for unit in (13, 14):
-            weave(unit, nc.scalar.copy)
-        quantise(4)
-        product(4, scales_late[:, 2 * C : 3 * C])
-        for unit in (15, 16, 17):
-            weave(unit, nc.scalar.copy)
-        quantise(5)
-        product(5, scales_late[:, 3 * C :])
-
-        last = 17 * UNIT_BYTES
-        square1 = on_bytes(last - half + 256, C, F32, "square1")
-        square(square1[:], relu1[:])
-        nc.vector.tensor_tensor(out_v[:].indirect(places(1, 1)), square1[:], gate_mid[:, :C], MULT)
-        late = on_bytes(last + 256, 4 * C, F32, "late")
-        relu(2, late[:, :C])
-        relu(3, late[:, C : 2 * C])
-        square(late[:, :C], late[:, :C])
-        square(late[:, C : 2 * C], late[:, C : 2 * C])
-        gated = on_bytes(2 * UNIT_BYTES, 2 * C, F32, "gated")
-        nc.vector.tensor_tensor(gated[:], late[:, : 2 * C], gate_mid[:, C:], MULT)
-        relu(4, late[:, 2 * C : 3 * C])
-        relu(5, late[:, 3 * C :])
-        square(late[:, 2 * C : 3 * C], late[:, 2 * C : 3 * C])
-        square(late[:, 3 * C :], late[:, 3 * C :])
-        nc.vector.tensor_tensor(out_v[:].indirect(places(4, 2)), late[:, 2 * C :], gate_last[:], MULT)
-        for i in range(2):
-            nc.scalar.activation(out_s[:].indirect(places(2 + i, 1)), gated[:, i * C : (i + 1) * C], ACT.Copy)
+        late_product(2)
+        late_product(3)
+        relu01 = on_unit(11, [2 * C], F32, "relu01")
+        square0 = on_unit(0, [C], F32, "square0")
+        relu(0, relu01[:, :C])
+        relu(1, relu01[:, C:])
+        square(square0[:], relu01[:, :C])
+        scatter_gated(0, C, square0[:], gate0[:])
+        late_product(4)
+        late_product(5)
+        late = on_bytes(14 * UNIT_BYTES + 4 * C, [5 * C], F32, "late")
+        square(late[:, :C], relu01[:, C:])
+        scatter_gated(C, SECOND, late[:, :SECOND], gate_mid[:, :SECOND])
+        share = sum(SHARES)
+        gated = on_unit(2, [share], F32, "gated")
+        for pair in ((2, 3), (4, 5)):
+            for e in pair:
+                relu(e, late[:, (e - 1) * C : e * C])
+            for e in pair:
+                square(late[:, (e - 1) * C : e * C], late[:, (e - 1) * C : e * C])
+            if pair == (2, 3):
+                nc.vector.tensor_tensor(gated[:], late[:, SECOND : SECOND + share], gate_mid[:, SECOND:], MULT)
+        scatter_gated(C + SECOND + share, 5 * C - SECOND - share, late[:, SECOND + share :], gate_last[:])
+        first = 0
+        for count in SHARES:
+            scatter_plain(C + SECOND + first, count, gated[:, first : first + count])
+            first += count
 
         first = 0
         for width in OUT_PIECES:

from contextlib import ExitStack

import concourse.mybir as mybir

K, T, E, C, N = 1536, 1536, 6, 256, 128
FLOPS = 2 * E * C * K * N

F32 = mybir.dt.float32
BF16 = mybir.dt.bfloat16
U32 = mybir.dt.uint32
I32 = mybir.dt.int32
U16 = mybir.dt.uint16
U8 = mybir.dt.uint8
FP8X4 = mybir.dt.float8_e4m3fn_x4
ACT = mybir.ActivationFunctionType
MULT = mybir.AluOpType.mult

P = 128
PACK = 4
K_PASS = P * PACK
PASSES = K // K_PASS
SCALE_ROWS = 4
LINE = 4
LIST_COLS = C // 16
WINDOW = 2048

X_LOADS = (
    (((512, 192), (512, 0), (256, 256), (256, 256)),),
    (((512, 512),), ((512, 512),), ((256, 256), (256, 64))),
    (((512, 512),), ((256, 256), (256, 128)), ((256, 256),), ((256, 96),)),
)
X_BUFS = 5

UNITS = E * PASSES
UNIT_BYTES = PACK * N * 4
ON_GPSIMD = (3, 4)
ON_VECTOR = (17,)
SECOND = 192
SHARES = (288, 256)
EARLY = 2
OUT_PIECES = (512, 512, 512)
ADD = mybir.AluOpType.add


def tile_moe_two_lin_relu2_kernel(tc, xT, w, b, gate, offs, dst, out):
    nc = tc.nc
    with ExitStack() as ctx:
        held = ctx.enter_context(tc.tile_pool(name="held", bufs=1))
        xraw = ctx.enter_context(tc.tile_pool(name="xraw", bufs=1))
        xgrp = ctx.enter_context(tc.tile_pool(name="xgrp", bufs=X_BUFS))
        shared = ctx.enter_context(tc.tile_pool(name="shared", bufs=1))
        psum = ctx.enter_context(tc.psum_pool(name="psum", bufs=1))

        def on_bytes(offset, shape, dtype, name):
            return shared.tile([P] + shape, dtype, name=name, offset=offset, align_bytes=64)

        def on_unit(unit, shape, dtype, name):
            return on_bytes(unit * UNIT_BYTES, shape, dtype, name)


        offs_sb = held.tile([P, T // 16], U16, name="offs_sb")
        dst_sb = held.tile([P, T // 16], U16, name="dst_sb")
        bias = held.tile([P, E], F32, name="bias")
        gate0 = held.tile([P, C], F32, name="gate0", align_bytes=256)
        gate_mid = held.tile([P, SECOND + sum(SHARES)], F32, name="gate_mid", align_bytes=256)
        gate_last = held.tile([P, 5 * C - SECOND - sum(SHARES)], F32, name="gate_last", align_bytes=256)
        out_v = held.tile([P, T], F32, name="out_v", align_bytes=256)
        out_s = held.tile([P, T], F32, name="out_s", align_bytes=256)
        x_scales = held.tile([P, T], U8, name="planes", align_bytes=64)
        x_words = [held.tile([P, WINDOW], U32, name=f"codes{a}", align_bytes=64) for a in range(PASSES)]
        slot_words = [held.tile([P, T], U32, name=f"g_codes{a}", align_bytes=64) for a in range(PASSES)]
        warm = held.tile([P, 1], F32, name="warm")

        nc.gpsimd.memset(x_scales[:].bitcast(I32), 0)
        for a in range(PASSES):
            nc.gpsimd.memset(x_words[a][:, T:].bitcast(I32), 0)
        nc.vector.memset(out_v[:], 0.0)
        nc.vector.memset(out_s[:], 0.0)
        nc.gpsimd.memset(warm[:], 0.0)
        nc.scalar.activation(warm[:], warm[:], ACT.Relu)

        x_tiles = [[] for a in range(PASSES)]
        for a in range(PASSES):
            rows = xT[a * K_PASS : (a + 1) * K_PASS, :].rearrange("(p j) t -> p j t", j=PACK)
            first = 0
            for i, tiles in enumerate(X_LOADS[a]):
                width = sum(tokens for tokens, share in tiles)
                raw = xraw.tile([P, PACK, width], F32, name=f"x{a}_{i}", align_bytes=256)
                if a == 0:
                    run = rows.rearrange("p j t -> p (j t)")
                    flat = raw[:].rearrange("p j t -> p (j t)")
                    cut = (PACK - 1) * T + tiles[0][0]
                    nc.sync.dma_start(out=flat[:, :cut], in_=run[:, :cut])
                    nc.sync.dma_start(out=flat[:, cut:], in_=run[:, cut:])
                else:
                    nc.sync.dma_start(out=raw[:], in_=rows[:, :, first : first + width])
                lo = 0
                for tokens, share in tiles:
                    x_tiles[a].append((raw[:, :, lo : lo + tokens], first + lo, tokens, share))
                    lo += tokens
                first += width
            if a == 0:
                nc.sync.dma_start(offs_sb[:], offs)

        w_units = w.rearrange("e (a p j) n -> p (e a) (j n)", p=P, j=PACK)
        w_raw = []
        for unit in range(UNITS):
            raw = on_unit(unit, [PACK * N], F32, f"w{unit}")
            nc.sync.dma_start(out=raw[:], in_=w_units[:, unit])
            w_raw.append(raw)
            if unit == 3:
                nc.sync.dma_start(out=bias[:], in_=b)
            if unit == 11:
                nc.sync.dma_start(dst_sb[:], dst)
                nc.sync.dma_start(out=gate0[:], in_=gate[:, :C])
        nc.sync.dma_start(out=gate_mid[:], in_=gate[:, C : C + SECOND + sum(SHARES)])
        nc.sync.dma_start(out=gate_last[:], in_=gate[:, C + SECOND + sum(SHARES) :])

        for a in range(PASSES):
            for src, first, tokens, share in x_tiles[a]:
                woven = xgrp.tile([P, tokens, PACK], BF16, name=f"grp{tokens}", align_bytes=64)
                to = woven[:].rearrange("p (c i) j -> p c j i", i=LINE)
                fr = src.rearrange("p j (c i) -> p c j i", i=LINE)
                mid = share // LINE
                if share:
                    nc.scalar.activation(to[:, :mid], fr[:, :mid], ACT.Copy)
                if share < tokens:
                    nc.vector.tensor_copy(to[:, mid:], fr[:, mid:])
                nc.vector.quantize_mx(
                    out=x_words[a][:, first : first + tokens].bitcast(FP8X4),
                    scales=x_scales[SCALE_ROWS * a : P, first : first + tokens],
                    in_=woven[:].rearrange("p t j -> p (t j)"),
                )
            nc.vector.tensor_copy(slot_words[a][:], x_words[a][:].indirect(offs_sb[:]))

        w_woven = [held.tile([P, PASSES, N, PACK], BF16, name=f"w_grp{e}", align_bytes=64) for e in range(E)]
        w_words = [held.tile([P, PASSES * N], U32, name=f"w_codes{e}", align_bytes=64) for e in range(E)]
        w_scales = [held.tile([P, PASSES * N], U8, name=f"w_planes{e}", align_bytes=64) for e in range(E)]

        def weave(unit):
            e, a = divmod(unit, PASSES)
            if unit in ON_GPSIMD:
                fr = w_raw[unit][:].rearrange("p (j n) -> p n j", j=PACK)
                nc.gpsimd.tensor_scalar(w_woven[e][:, a], fr, 1.0, 0.0, MULT, ADD)
            else:
                to = w_woven[e][:, a].rearrange("p (c i) j -> p c j i", i=LINE)
                fr = w_raw[unit][:].rearrange("p (j c i) -> p c j i", j=PACK, i=LINE)
                copy = nc.vector.tensor_copy if unit in ON_VECTOR else nc.scalar.copy
                copy(to, fr)

        def quantise(e):
            for lo, hi in ((0, 2), (2, 3)) if e == E - 1 else ((0, 3),):
                nc.vector.quantize_mx(
                    out=w_words[e][:, lo * N : hi * N].bitcast(FP8X4),
                    scales=w_scales[e][:, lo * N : hi * N],
                    in_=w_woven[e][:, lo:hi].rearrange("p u n j -> p (u n j)"),
                )

        acc = [psum.tile([P, C], F32, name=f"acc{e}") for e in range(E)]

        def product(e, scales):
            for a in range(PASSES):
                words = slot_words[a][:, e * C : (e + 1) * C]
                nc.tensor.matmul_mx(
                    out=acc[e][:],
                    lhsT=w_words[e][:, a * N : (a + 1) * N].bitcast(FP8X4),
                    lhsT_scale=w_scales[e][:, a * N : (a + 1) * N],
                    rhs=words.bitcast(FP8X4),
                    rhs_scale=scales[SCALE_ROWS * a : P],
                    start=(a == 0),
                    stop=(a == PASSES - 1),
                )

        def relu(e, to):
            nc.scalar.activation(to, acc[e][:], ACT.Relu, bias=bias[:, e : e + 1])

        def square(to, fr):
            nc.scalar.activation(to, fr, ACT.Square)

        def entries(lists, first, count):
            return lists[:, first // 16 : (first + count) // 16]

        def gather(to, window, first, count):
            nc.vector.tensor_copy(to, window[:].indirect(entries(offs_sb, first, count)))

        def scatter_gated(first, count, values, gates):
            nc.vector.tensor_tensor(out_v[:].indirect(entries(dst_sb, first, count)), values, gates, MULT)

        def scatter_plain(first, count, values):
            nc.scalar.activation(out_s[:].indirect(entries(dst_sb, first, count)), values, ACT.Copy)

        scales_early = held.tile([P, EARLY * C], U8, name="scales_early", align_bytes=64)
        gather(scales_early[:], x_scales, 0, EARLY * C)
        for e in range(EARLY):
            for unit in range(e * PASSES, (e + 1) * PASSES):
                weave(unit)
            quantise(e)
            product(e, scales_early[:, e * C : (e + 1) * C])
        scales_late = on_bytes(5 * UNIT_BYTES - 512, [(E - EARLY) * C], U8, "scales_late")
        gather(scales_late[:], x_scales, EARLY * C, (E - EARLY) * C)

        def late_product(e):
            for unit in range(e * PASSES, (e + 1) * PASSES):
                weave(unit)
            quantise(e)
            product(e, scales_late[:, (e - EARLY) * C : (e - EARLY + 1) * C])

        late_product(2)
        late_product(3)
        relu01 = on_unit(11, [2 * C], F32, "relu01")
        square0 = on_unit(0, [C], F32, "square0")
        relu(0, relu01[:, :C])
        relu(1, relu01[:, C:])
        square(square0[:], relu01[:, :C])
        scatter_gated(0, C, square0[:], gate0[:])
        late_product(4)
        late_product(5)
        late = on_bytes(14 * UNIT_BYTES + 4 * C, [5 * C], F32, "late")
        square(late[:, :C], relu01[:, C:])
        scatter_gated(C, SECOND, late[:, :SECOND], gate_mid[:, :SECOND])
        share = sum(SHARES)
        gated = on_unit(2, [share], F32, "gated")
        for pair in ((2, 3), (4, 5)):
            for e in pair:
                relu(e, late[:, (e - 1) * C : e * C])
            for e in pair:
                square(late[:, (e - 1) * C : e * C], late[:, (e - 1) * C : e * C])
            if pair == (2, 3):
                nc.vector.tensor_tensor(gated[:], late[:, SECOND : SECOND + share], gate_mid[:, SECOND:], MULT)
        scatter_gated(C + SECOND + share, 5 * C - SECOND - share, late[:, SECOND + share :], gate_last[:])
        first = 0
        for count in SHARES:
            scatter_plain(C + SECOND + first, count, gated[:, first : first + count])
            first += count

        first = 0
        for width in OUT_PIECES:
            piece = slice(first, first + width)
            nc.vector.tensor_tensor(out_v[:, piece], out_v[:, piece], out_s[:, piece], ADD)
            nc.sync.dma_start(out=out[:, piece], in_=out_v[:, piece])
            first += width
